import numpy as np
import ml_dtypes


def mxq(x, axis, fmt="e4m3"):
    dtype, down = {"e4m3": (ml_dtypes.float8_e4m3fn, 7), "e5m2": (ml_dtypes.float8_e5m2, 14)}[fmt]
    v = np.moveaxis(np.asarray(x, np.float32).astype(ml_dtypes.bfloat16).astype(np.float64), axis, -1)
    blocks = v.reshape(v.shape[:-1] + (-1, 32))
    amax = np.abs(blocks).max(-1, keepdims=True)
    byte = np.maximum(np.where(amax > 0, np.frexp(amax)[1] - 1 + 127, 0) - down, 1)
    scale = np.exp2(byte - 127.0)
    codes = (blocks / scale).astype(np.float32).astype(dtype).astype(np.float64)
    return np.moveaxis((codes * scale).reshape(v.shape), -1, axis)


WIDE = False


def mx_kscale(k):
    if not WIDE:
        return np.ones(k)
    levels = np.array([10, -10, 5, -5, 0])
    if k % 512:
        return np.exp2(np.random.permutation(np.resize(levels, k // 32))).repeat(32)
    a = np.empty((k // 512, 16))
    for p in range(k // 512):
        a[p, :8] = np.random.permutation(np.resize(levels, 8))
        for g in range(8):
            far = levels[np.abs(levels - a[p, g]) >= 10]
            a[p, g + 8] = far[np.random.randint(len(far))]
    return np.exp2(a.ravel()).repeat(32)


def f64(x):
    return np.asarray(x).astype(np.float64)


def striped(idx):
    return np.tile(idx.reshape(-1, 16).T, (8, 1)).astype(np.uint16)


def unstriped(offs):
    return offs[:16].T.reshape(-1).astype(np.int64)


E2M1 = np.array([0.0, 0.5, 1.0, 1.5, 2.0, 3.0, 4.0, 6.0, -0.0, -0.5, -1.0, -1.5, -2.0, -3.0, -4.0, -6.0])


def pack_weight(w, fmt):
    k, n = w.shape
    w = f64(np.asarray(w, np.float32).astype(ml_dtypes.bfloat16)).reshape(k // 32, 32, n)
    amax = np.abs(w).max(1)
    if fmt == "e4m3":
        byte = np.frexp(amax)[1] - 1 + 127 - 7
    else:
        mant, ex = np.frexp(amax / 6.0)
        byte = np.where(mant > 0.5, ex, ex - 1) + 127
    byte = np.clip(np.where(amax > 0, byte, 1), 1, 254)
    scaled = (w * np.exp2(127.0 - byte)[:, None, :]).reshape(k, n).astype(np.float32)
    by_word = np.ascontiguousarray(scaled.reshape(k // 512, 128, 4, n).transpose(0, 1, 3, 2))
    if fmt == "e4m3":
        words = by_word.astype(ml_dtypes.float8_e4m3fn).view(np.uint8)
    else:
        c = by_word.astype(ml_dtypes.float4_e2m1fn).view(np.uint8) & 0xF
        words = (c[..., 0::2] | (c[..., 1::2] << 4)).reshape(k // 512, 128, 2 * n)
    return np.ascontiguousarray(words), np.ascontiguousarray(byte.astype(np.uint8).reshape(k // 512, 16, n))


def unpack_weight(words, scales, fmt):
    g, _, n = scales.shape
    words = np.ascontiguousarray(words).reshape(g, 128, n, -1)
    if fmt == "e4m3":
        vals = words.view(ml_dtypes.float8_e4m3fn).astype(np.float64)
    else:
        nib = np.empty((g, 128, n, 4), np.uint8)
        nib[..., 0::2] = words & 0xF
        nib[..., 1::2] = words >> 4
        vals = E2M1[nib]
    vals = vals * np.repeat(np.exp2(scales.astype(np.float64) - 127.0), 8, axis=1)[..., None]
    return vals.transpose(0, 1, 3, 2).reshape(g * 512, n)


def gelu(v):
    return 0.5 * v * (1.0 + np.tanh(np.sqrt(2.0 / np.pi) * (v + 0.044715 * v**3)))


K, H, N, T, S = 1024, 512, 1280, 2048, 1024

def setup_inputs():
    n = np.random.standard_normal
    s = mx_kscale(K)[:, None]
    u = mx_kscale(H)
    tab_words, tab_scales = pack_weight(n((K, T)) * s, "e4m3")
    wc_words, wc_scales = pack_weight(n((K, H)) / K ** 0.5 / s, "e2m1")
    wj_words, wj_scales = pack_weight(1.5 * n((H, N)) / H ** 0.5 / u[:, None], "e4m3")
    return {
        "tab_words": tab_words, "tab_scales": tab_scales,
        "offs": striped(np.random.permutation(T)[:S]),
        "wc_words": wc_words, "wc_scales": wc_scales,
        "wf": (0.3 * n((K, H)) / K ** 0.5 / s).astype(np.float32),
        "enc": (0.5 * n(H)).astype(np.float32),
        "gain": (np.exp(0.2 * n(H)) * u).astype(np.float32),
        "wj_words": wj_words, "wj_scales": wj_scales,
        "bias": (0.3 * n(N)).astype(np.float32),
    }

def reference(tab_words, tab_scales, offs, wc_words, wc_scales, wf, enc, gain, wj_words, wj_scales, bias):
    v = unpack_weight(tab_words, tab_scales, "e4m3")[:, unstriped(offs)]
    wc = unpack_weight(wc_words, wc_scales, "e2m1")
    wfq = mxq(f64(wf), 0, "e4m3")
    wj = unpack_weight(wj_words, wj_scales, "e4m3")
    p = wc.T @ v + wfq.T @ v
    h = f64(gain)[:, None] * np.tanh(p + f64(enc)[:, None])
    hq = mxq(h, 0, "e4m3")
    return (wj.T @ hq) + f64(bias)[:, None]

@@ -1,0 +1,258 @@
+from contextlib import ExitStack
+
+import concourse.mybir as mybir
+from concourse.masks import make_identity
+
+K, H, N, T, S = 1024, 512, 1280, 2048, 1024
+FLOPS = 2 * S * (2 * K * H + H * N)
+
+F32 = mybir.dt.float32
+BF16 = mybir.dt.bfloat16
+I32 = mybir.dt.int32
+U32 = mybir.dt.uint32
+U16 = mybir.dt.uint16
+U8 = mybir.dt.uint8
+FP8X4 = mybir.dt.float8_e4m3fn_x4
+FP4X4 = mybir.dt.float4_e2m1fn_x4
+ACT = mybir.ActivationFunctionType
+ALU = mybir.AluOpType
+
+P = 128
+PASSES = 2
+CHUNK = 512
+PIECES = [(0, 256), (256, 256), (512, 256), (768, 256)]
+N_TILES = N // P
+
+
+def tile_list_transducer_joint_logits_kernel(
+    tc, tab_words, tab_scales, offs, wc_words, wc_scales, wf, enc, gain, wj_words, wj_scales, bias, out
+):
+    nc = tc.nc
+    with ExitStack() as ctx:
+        held = ctx.enter_context(tc.tile_pool(name="held", bufs=1))
+        work = ctx.enter_context(tc.tile_pool(name="work", bufs=2))
+        stage = ctx.enter_context(tc.tile_pool(name="stage", bufs=6))
+        psum = ctx.enter_context(tc.psum_pool(name="psum", bufs=8))
+
+        offsets = held.tile([P, S // 16], U16, name="offsets")
+        late = ctx.enter_context(tc.tile_pool(name="late", bufs=1))
+        tab_s = held.tile([P, PASSES * T // 4], I32, name="tab_s", align_bytes=64)
+        wc_s_raw = held.tile([P, PASSES * H // 4], I32, name="wc_s_raw", align_bytes=64)
+        warm = late.tile([P, (2048 + 3 * 8192 + 128) // 4], F32, name="warm", align_bytes=64, offset=0)
+        bias_rows = held.tile([P, P], F32, name="bias_rows")
+        ident = held.tile([P, P], F32, name="ident")
+        nc.vector.memset(bias_rows[:], 0.0)
+        nc.scalar.dma_start(out=bias_rows[0:N_TILES, :], in_=bias.rearrange("(u p) -> u p", p=P))
+        nc.vector.memset(tab_s[:], 0)
+        make_identity(nc, ident[:])
+        nc.gpsimd.memset(wc_s_raw[:], 0)
+        nc.vector.memset(warm[:, 0:1], 0.0)
+        nc.scalar.activation(warm[:, 1:2], warm[:, 0:1], ACT.Tanh)
+
+        def load_scale_rows(queue, dst, src):
+            rows = src.bitcast(I32).rearrange("a (q r) c -> r q a c", r=4)
+            for r in range(4):
+                queue.dma_start(out=dst[r:P:32, :].rearrange("q (a c) -> q a c", a=src.shape[0]), in_=rows[r])
+
+        def table_words(a):
+            return tab_words[a].rearrange("p t i -> p (t i)").bitcast(I32)
+
+        nc.sync.dma_start(offsets[:], offs)
+        first = ctx.enter_context(tc.tile_pool(name="first", bufs=1))
+        tab_w0 = first.tile([P, T], I32, name="tab_w0", tag="tab0_then_wj", align_bytes=64)
+        nc.sync.dma_start(out=tab_w0[:], in_=table_words(0))
+        load_scale_rows(nc.sync, tab_s, tab_scales)
+        load_scale_rows(nc.gpsimd, wc_s_raw, wc_scales)
+        wc_raw = late.tile([P, PASSES, H // 2], I32, name="wc_raw", align_bytes=64, offset=0)
+        nc.sync.dma_start(out=wc_raw[:], in_=wc_words.bitcast(I32).rearrange("a p c -> p a c"))
+        tab_w1 = late.tile([P, T], I32, name="tab_w1", align_bytes=64, offset=2048)
+        nc.sync.dma_start(out=tab_w1[:], in_=table_words(1))
+        tab_w = [tab_w0, tab_w1]
+        wf_raw = []
+        for a in range(PASSES):
+            w = late.tile([P, 4, H], F32, name="wf_raw%d" % a, align_bytes=64, offset=2048 + 8192 * (a + 1))
+            nc.sync.dma_start(out=w[:], in_=wf[512 * a : 512 * (a + 1), :].rearrange("(p j) c -> p j c", j=4))
+            wf_raw.append(w)
+        enc_sb = late.tile([P, 4], F32, name="enc_sb", align_bytes=64, offset=2048 + 3 * 8192)
+        gain_sb = late.tile([P, 4], F32, name="gain_sb", align_bytes=64, offset=2048 + 3 * 8192 + 64)
+        nc.sync.dma_start(out=enc_sb[:], in_=enc.rearrange("(p t) -> p t", t=4))
+        nc.sync.dma_start(out=gain_sb[:], in_=gain.rearrange("(p t) -> p t", t=4))
+        bias_ps = psum.tile([P, P], F32, name="bank", tag="bank")
+        nc.tensor.transpose(bias_ps[:], bias_rows[:], ident[:])
+        bias_sb = held.tile([P, N_TILES], F32, name="bias_sb")
+        nc.scalar.copy(out=bias_sb[:], in_=bias_ps[:, 0:N_TILES])
+
+        v_s = {}
+        v_w = {}
+
+        def gather_scales(a, c):
+            g = held.tile([P, CHUNK], U8, name="v_s%d%d" % (a, c), align_bytes=64)
+            window = tab_s[:].bitcast(U8)[:, a * T : (a + 1) * T]
+            nc.vector.tensor_copy(g[:], window.indirect(offsets[:, 32 * c : 32 * (c + 1)]))
+            v_s[a, c] = g
+
+        def gather_words(a, c):
+            g = held.tile([P, CHUNK], U32, name="v_w%d%d" % (a, c), align_bytes=64)
+            nc.vector.tensor_copy(g[:], tab_w[a][:].bitcast(U32).indirect(offsets[:, 32 * c : 32 * (c + 1)]))
+            v_w[a, c] = g
+
+        wc_w = held.tile([P, PASSES, 4, 2 * P], U8, name="wc_w", align_bytes=64)
+        wc_s = held.tile([P, PASSES, 4, P], U8, name="wc_s", align_bytes=64)
+
+        def permute_wc(a):
+            nc.vector.tensor_copy(
+                out=wc_w[:, a, :, :].bitcast(U16),
+                in_=wc_raw[:, a, :].bitcast(U16).rearrange("p (m t) -> p t m", t=4),
+            )
+            nc.vector.tensor_copy(
+                out=wc_s[:, a, :, :],
+                in_=wc_s_raw[:].bitcast(U8)[:, a * H : (a + 1) * H].rearrange("p (m t) -> p t m", t=4),
+            )
+
+        wf_bf = [held.tile([P, 4, P, 4], BF16, name="wf_bf%d" % a, align_bytes=64) for a in range(PASSES)]
+        wf_w = held.tile([P, PASSES, 4, P], U32, name="wf_w", align_bytes=64)
+        wf_s = held.tile([P, PASSES, 4, P], U8, name="wf_s", align_bytes=64)
+
+        def cast_wf(copy, a, t0, t1):
+            copy(
+                out=wf_bf[a][:, t0:t1, :, :].rearrange("p t m j -> p m t j"),
+                in_=wf_raw[a][:].rearrange("p j (m t) -> p m t j", t=4)[:, :, t0:t1, :],
+            )
+
+        def quantize_wf(a, t0, t1):
+            nc.vector.quantize_mx(
+                out=wf_w[:, a, t0:t1, :].rearrange("p t m -> p (t m)").bitcast(FP8X4),
+                scales=wf_s[:, a, t0:t1, :].rearrange("p t m -> p (t m)"),
+                in_=wf_bf[a][:, t0:t1, :, :].rearrange("p t m j -> p (t m j)"),
+            )
+
+        acc = {}
+
+        def coarse(a, c):
+            for t in range(4):
+                if a == 0:
+                    acc[c, t] = psum.tile([P, CHUNK], F32, name="bank", tag="bank")
+                nc.tensor.matmul_mx(
+                    out=acc[c, t][:],
+                    lhsT=wc_w[:, a, t, :].bitcast(FP4X4),
+                    lhsT_scale=wc_s[:, a, t, :],
+                    rhs=v_w[a, c][:].bitcast(FP8X4),
+                    rhs_scale=v_s[a, c][:],
+                    start=(a == 0),
+                    stop=False,
+                )
+
+        def fine(a, c):
+            for t in range(4):
+                nc.tensor.matmul_mx(
+                    out=acc[c, t][:],
+                    lhsT=wf_w[:, a, t, :].bitcast(FP8X4),
+                    lhsT_scale=wf_s[:, a, t, :],
+                    rhs=v_w[a, c][:].bitcast(FP8X4),
+                    rhs_scale=v_s[a, c][:],
+                    start=False,
+                    stop=(a == PASSES - 1),
+                )
+
+        gather_words(0, 0)
+        gather_scales(0, 0)
+        permute_wc(0)
+        coarse(0, 0)
+        gather_words(0, 1)
+        gather_scales(0, 1)
+        coarse(0, 1)
+        permute_wc(1)
+        wj_w = first.tile([P, N], I32, name="wj_w", tag="tab0_then_wj", align_bytes=64)
+        wj_s = late.tile([P, N // 4], I32, name="wj_s", align_bytes=64, offset=0)
+        nc.vector.memset(wj_s[:], 0)
+        load_scale_rows(nc.sync, wj_s, wj_scales)
+        nc.sync.dma_start(out=wj_w[:], in_=wj_words[0].rearrange("p c i -> p (c i)").bitcast(I32))
+        gather_words(1, 0)
+        gather_scales(1, 0)
+        coarse(1, 0)
+        cast_wf(nc.scalar.copy, 0, 0, 4)
+        quantize_wf(0, 0, 4)
+        fine(0, 0)
+        fine(0, 1)
+        cast_wf(nc.vector.tensor_copy, 1, 0, 2)
+        cast_wf(nc.scalar.copy, 1, 2, 4)
+        quantize_wf(1, 0, 2)
+        quantize_wf(1, 2, 4)
+        fine(1, 0)
+        gather_words(1, 1)
+        gather_scales(1, 1)
+        coarse(1, 1)
+        fine(1, 1)
+
+        th = {}
+        hq = {}
+
+        def join_tanh(i):
+            j0, n = PIECES[i]
+            c, o = divmod(j0, CHUNK)
+            th[i] = work.tile([P, 4, n], F32, name="th", tag="th", align_bytes=64)
+            for t in range(4):
+                nc.scalar.activation(th[i][:, t, :], acc[c, t][:, o : o + n], ACT.Tanh, bias=enc_sb[:, t : t + 1])
+
+        def join_gain(i):
+            n = PIECES[i][1]
+            hb = work.tile([P, n, 4], BF16, name="hb", tag="hb", align_bytes=64)
+            nc.vector.tensor_tensor(
+                out=hb[:],
+                in0=th[i][:].rearrange("p t n -> p n t"),
+                in1=gain_sb[:].unsqueeze(1).to_broadcast([P, n, 4]),
+                op=ALU.mult,
+            )
+            h_w = held.tile([P, n], U32, name="h_w%d" % i, align_bytes=64)
+            h_s = held.tile([P, n], U8, name="h_s%d" % i, align_bytes=64)
+            nc.vector.quantize_mx(out=h_w[:].bitcast(FP8X4), scales=h_s[:], in_=hb[:].rearrange("p n t -> p (n t)"))
+            hq[i] = (h_w, h_s)
+
+        def logits(i, on_vector):
+            j0, n = PIECES[i]
+            h_w, h_s = hq[i]
+            per_bank = CHUNK // n
+            for b in range(N_TILES // per_bank):
+                bank = psum.tile([P, per_bank, n], F32, name="bank", tag="bank")
+                res = stage.tile([P, per_bank, n], F32, name="res", tag="res")
+                for e in range(per_bank):
+                    u = b * per_bank + e
+                    nc.tensor.matmul_mx(
+                        out=bank[:, e, :],
+                        lhsT=wj_w[:, u * P : (u + 1) * P].bitcast(FP8X4),
+                        lhsT_scale=wj_s[:].bitcast(U8)[:, u * P : (u + 1) * P],
+                        rhs=h_w[:].bitcast(FP8X4),
+                        rhs_scale=h_s[:],
+                        start=True,
+                        stop=True,
+                    )
+                u0 = b * per_bank
+                if b in on_vector:
+                    nc.vector.tensor_tensor(
+                        out=res[:],
+                        in0=bank[:],
+                        in1=bias_sb[:, u0 : u0 + per_bank].unsqueeze(2).to_broadcast([P, per_bank, n]),
+                        op=ALU.add,
+                    )
+                else:
+                    for e in range(per_bank):
+                        nc.scalar.activation(
+                            res[:, e, :], bank[:, e, :], ACT.Identity, bias=bias_sb[:, u0 + e : u0 + e + 1]
+                        )
+                nc.sync.dma_start(
+                    out=out[u0 * P : (u0 + per_bank) * P, j0 : j0 + n].rearrange("(e p) j -> p e j", p=P),
+                    in_=res[:],
+                )
+
+        join_tanh(0)
+        join_gain(0)
+        join_tanh(1)
+        logits(0, (0, 2))
+        join_gain(1)
+        join_tanh(2)
+        logits(1, (1, 3))
+        join_gain(2)
+        join_tanh(3)
+        logits(2, (1, 3))
+        join_gain(3)
+        logits(3, (0, 2, 4))

@@ -20,7 +20,7 @@ ALU = mybir.AluOpType
 P = 128
 PASSES = 2
 CHUNK = 512
-PIECES = [(0, 256), (256, 256), (512, 256), (768, 256)]
+PIECES = [(0, 128), (128, 128), (256, 256), (512, 256), (768, 256)]
 N_TILES = N // P
 
 
@@ -30,69 +30,75 @@ def tile_list_transducer_joint_logits_kernel(
     nc = tc.nc
     with ExitStack() as ctx:
         held = ctx.enter_context(tc.tile_pool(name="held", bufs=1))
-        work = ctx.enter_context(tc.tile_pool(name="work", bufs=2))
-        stage = ctx.enter_context(tc.tile_pool(name="stage", bufs=6))
-        psum = ctx.enter_context(tc.psum_pool(name="psum", bufs=8))
+        work = ctx.enter_context(tc.tile_pool(name="work", bufs=3))
+        stage = ctx.enter_context(tc.tile_pool(name="stage", bufs=10))
+        psum = ctx.enter_context(tc.psum_pool(name="psum", bufs=1))
 
         offsets = held.tile([P, S // 16], U16, name="offsets")
-        late = ctx.enter_context(tc.tile_pool(name="late", bufs=1))
-        tab_s = held.tile([P, PASSES * T // 4], I32, name="tab_s", align_bytes=64)
+        ring = ctx.enter_context(tc.tile_pool(name="ring", bufs=1))
+        tab_s = ring.tile([P, T // 4], I32, name="tab_s", align_bytes=64, offset=16384)
         wc_s_raw = held.tile([P, PASSES * H // 4], I32, name="wc_s_raw", align_bytes=64)
-        warm = late.tile([P, (2048 + 3 * 8192 + 128) // 4], F32, name="warm", align_bytes=64, offset=0)
-        bias_rows = held.tile([P, P], F32, name="bias_rows")
+        wj_s = held.tile([P, N // 4], I32, name="wj_s", align_bytes=64)
+        warm = held.tile([P, 2], F32, name="warm")
+        v_s1 = held.tile([P, S // 4], I32, name="v_s1", align_bytes=64)
         ident = held.tile([P, P], F32, name="ident")
-        nc.vector.memset(bias_rows[:], 0.0)
+        bias_rows = held.tile([P, P], F32, name="bias_rows")
+        nc.gpsimd.memset(bias_rows[:], 0.0)
         nc.scalar.dma_start(out=bias_rows[0:N_TILES, :], in_=bias.rearrange("(u p) -> u p", p=P))
-        nc.vector.memset(tab_s[:], 0)
-        make_identity(nc, ident[:])
         nc.gpsimd.memset(wc_s_raw[:], 0)
+        nc.vector.memset(tab_s[:], 0)
+        nc.vector.memset(v_s1[:], 0)
+        nc.vector.memset(wj_s[:], 0)
         nc.vector.memset(warm[:, 0:1], 0.0)
+        make_identity(nc, ident[:])
         nc.scalar.activation(warm[:, 1:2], warm[:, 0:1], ACT.Tanh)
 
-        def load_scale_rows(queue, dst, src):
+        def load_scale_rows(dst, src):
             rows = src.bitcast(I32).rearrange("a (q r) c -> r q a c", r=4)
             for r in range(4):
-                queue.dma_start(out=dst[r:P:32, :].rearrange("q (a c) -> q a c", a=src.shape[0]), in_=rows[r])
+                nc.sync.dma_start(out=dst[r:P:32, :].rearrange("q (a c) -> q a c", a=src.shape[0]), in_=rows[r])
 
-        def table_words(a):
-            return tab_words[a].rearrange("p t i -> p (t i)").bitcast(I32)
+        def load_table_words(a):
+            t_w = held.tile([P, T], I32, name="tab_w%d" % a, align_bytes=64)
+            nc.sync.dma_start(out=t_w[:], in_=tab_words[a].rearrange("p t i -> p (t i)").bitcast(I32))
+            return t_w
+
+        def load_wf(a):
+            w = ring.tile([P, 4, H], F32, name="wf_raw%d" % a, align_bytes=64, offset=8192 * a)
+            nc.sync.dma_start(out=w[:], in_=wf[512 * a : 512 * (a + 1), :].rearrange("(p j) c -> p j c", j=4))
+            return w
 
         nc.sync.dma_start(offsets[:], offs)
-        first = ctx.enter_context(tc.tile_pool(name="first", bufs=1))
-        tab_w0 = first.tile([P, T], I32, name="tab_w0", tag="tab0_then_wj", align_bytes=64)
-        nc.sync.dma_start(out=tab_w0[:], in_=table_words(0))
-        load_scale_rows(nc.sync, tab_s, tab_scales)
-        load_scale_rows(nc.gpsimd, wc_s_raw, wc_scales)
-        wc_raw = late.tile([P, PASSES, H // 2], I32, name="wc_raw", align_bytes=64, offset=0)
+        wc_raw = held.tile([P, PASSES, H // 2], I32, name="wc_raw", align_bytes=64)
         nc.sync.dma_start(out=wc_raw[:], in_=wc_words.bitcast(I32).rearrange("a p c -> p a c"))
-        tab_w1 = late.tile([P, T], I32, name="tab_w1", align_bytes=64, offset=2048)
-        nc.sync.dma_start(out=tab_w1[:], in_=table_words(1))
-        tab_w = [tab_w0, tab_w1]
-        wf_raw = []
-        for a in range(PASSES):
-            w = late.tile([P, 4, H], F32, name="wf_raw%d" % a, align_bytes=64, offset=2048 + 8192 * (a + 1))
-            nc.sync.dma_start(out=w[:], in_=wf[512 * a : 512 * (a + 1), :].rearrange("(p j) c -> p j c", j=4))
-            wf_raw.append(w)
-        enc_sb = late.tile([P, 4], F32, name="enc_sb", align_bytes=64, offset=2048 + 3 * 8192)
-        gain_sb = late.tile([P, 4], F32, name="gain_sb", align_bytes=64, offset=2048 + 3 * 8192 + 64)
-        nc.sync.dma_start(out=enc_sb[:], in_=enc.rearrange("(p t) -> p t", t=4))
-        nc.sync.dma_start(out=gain_sb[:], in_=gain.rearrange("(p t) -> p t", t=4))
-        bias_ps = psum.tile([P, P], F32, name="bank", tag="bank")
-        nc.tensor.transpose(bias_ps[:], bias_rows[:], ident[:])
-        bias_sb = held.tile([P, N_TILES], F32, name="bias_sb")
-        nc.scalar.copy(out=bias_sb[:], in_=bias_ps[:, 0:N_TILES])
+        load_scale_rows(wc_s_raw, wc_scales)
+        tab_w = [load_table_words(0)]
+        for q in range(4):
+            nc.sync.dma_start(out=tab_s[32 * q : 32 * q + 8, :], in_=tab_scales.bitcast(I32)[:, 4 * q : 4 * q + 4, :])
+        wf_raw = [load_wf(0)]
+        tab_w.append(load_table_words(1))
+        wf_raw.append(load_wf(1))
 
         v_s = {}
         v_w = {}
 
-        def gather_scales(a, c):
-            g = held.tile([P, CHUNK], U8, name="v_s%d%d" % (a, c), align_bytes=64)
-            window = tab_s[:].bitcast(U8)[:, a * T : (a + 1) * T]
-            nc.vector.tensor_copy(g[:], window.indirect(offsets[:, 32 * c : 32 * (c + 1)]))
-            v_s[a, c] = g
+        v_s01 = held.tile([P, S], U8, name="v_s01", align_bytes=64)
+
+        def gather_scales(c):
+            cols = slice(c * CHUNK, (c + 1) * CHUNK)
+            nc.vector.tensor_copy(v_s01[:, cols], tab_s[:].bitcast(U8).indirect(offsets[:, 32 * c : 32 * (c + 1)]))
+            v_s[0, c] = v_s01[:, cols]
+            v_s[1, c] = v_s1[:].bitcast(U8)[:, cols]
+
+        def shift_scales():
+            for r in range(4):
+                nc.sync.dma_start(out=v_s1[r:P:32, :], in_=v_s01[:].bitcast(I32)[4 + r : P : 32, :])
 
         def gather_words(a, c):
-            g = held.tile([P, CHUNK], U32, name="v_w%d%d" % (a, c), align_bytes=64)
+            if c == 1:
+                g = ring.tile([P, CHUNK], U32, name="v_w%d1" % a, align_bytes=64, offset=(16384, 8192)[a])
+            else:
+                g = held.tile([P, CHUNK], U32, name="v_w%d0" % a, align_bytes=64)
             nc.vector.tensor_copy(g[:], tab_w[a][:].bitcast(U32).indirect(offsets[:, 32 * c : 32 * (c + 1)]))
             v_w[a, c] = g
 
@@ -128,16 +134,16 @@ def tile_list_transducer_joint_logits_kernel(
 
         acc = {}
 
-        def coarse(a, c):
-            for t in range(4):
+        def coarse(a, c, tiles=range(4)):
+            for t in tiles:
                 if a == 0:
-                    acc[c, t] = psum.tile([P, CHUNK], F32, name="bank", tag="bank")
+                    acc[c, t] = psum.tile([P, CHUNK], F32, name="acc", tag="bank%d" % ((4 * c + t) % 7))
                 nc.tensor.matmul_mx(
                     out=acc[c, t][:],
                     lhsT=wc_w[:, a, t, :].bitcast(FP4X4),
                     lhsT_scale=wc_s[:, a, t, :],
                     rhs=v_w[a, c][:].bitcast(FP8X4),
-                    rhs_scale=v_s[a, c][:],
+                    rhs_scale=v_s[a, c],
                     start=(a == 0),
                     stop=False,
                 )
@@ -149,40 +155,42 @@ def tile_list_transducer_joint_logits_kernel(
                     lhsT=wf_w[:, a, t, :].bitcast(FP8X4),
                     lhsT_scale=wf_s[:, a, t, :],
                     rhs=v_w[a, c][:].bitcast(FP8X4),
-                    rhs_scale=v_s[a, c][:],
+                    rhs_scale=v_s[a, c],
                     start=False,
                     stop=(a == PASSES - 1),
                 )
 
-        gather_words(0, 0)
-        gather_scales(0, 0)
         permute_wc(0)
-        coarse(0, 0)
-        gather_words(0, 1)
-        gather_scales(0, 1)
-        coarse(0, 1)
         permute_wc(1)
-        wj_w = first.tile([P, N], I32, name="wj_w", tag="tab0_then_wj", align_bytes=64)
-        wj_s = late.tile([P, N // 4], I32, name="wj_s", align_bytes=64, offset=0)
-        nc.vector.memset(wj_s[:], 0)
-        load_scale_rows(nc.sync, wj_s, wj_scales)
+        bias_ps = psum.tile([P, P], F32, name="bias_ps", tag="bank7")
+        nc.tensor.transpose(bias_ps[:], bias_rows[:], ident[:])
+        bias_sb = held.tile([P, N_TILES], F32, name="bias_sb")
+        nc.scalar.copy(out=bias_sb[:], in_=bias_ps[:, 0:N_TILES])
+        gather_words(0, 0)
+        gather_scales(0)
+        gather_scales(1)
+        shift_scales()
+        enc_sb = held.tile([P, 4], F32, name="enc_sb")
+        gain_sb = held.tile([P, 4], F32, name="gain_sb")
+        nc.sync.dma_start(out=enc_sb[:], in_=enc.rearrange("(p t) -> p t", t=4))
+        nc.sync.dma_start(out=gain_sb[:], in_=gain.rearrange("(p t) -> p t", t=4))
+        wj_w = held.tile([P, N], I32, name="wj_w", align_bytes=64)
         nc.sync.dma_start(out=wj_w[:], in_=wj_words[0].rearrange("p c i -> p (c i)").bitcast(I32))
-        gather_words(1, 0)
-        gather_scales(1, 0)
-        coarse(1, 0)
+        load_scale_rows(wj_s, wj_scales)
+        coarse(0, 0)
         cast_wf(nc.scalar.copy, 0, 0, 4)
         quantize_wf(0, 0, 4)
         fine(0, 0)
-        fine(0, 1)
+        gather_words(1, 0)
+        coarse(1, 0)
         cast_wf(nc.vector.tensor_copy, 1, 0, 2)
         cast_wf(nc.scalar.copy, 1, 2, 4)
         quantize_wf(1, 0, 2)
         quantize_wf(1, 2, 4)
         fine(1, 0)
+        gather_words(0, 1)
+        coarse(0, 1, range(3))
         gather_words(1, 1)
-        gather_scales(1, 1)
-        coarse(1, 1)
-        fine(1, 1)
 
         th = {}
         hq = {}
@@ -208,15 +216,15 @@ def tile_list_transducer_joint_logits_kernel(
             nc.vector.quantize_mx(out=h_w[:].bitcast(FP8X4), scales=h_s[:], in_=hb[:].rearrange("p n t -> p (n t)"))
             hq[i] = (h_w, h_s)
 
-        def logits(i, on_vector):
+        def logits(i, on_vector, banks):
             j0, n = PIECES[i]
             h_w, h_s = hq[i]
-            per_bank = CHUNK // n
-            for b in range(N_TILES // per_bank):
-                bank = psum.tile([P, per_bank, n], F32, name="bank", tag="bank")
+            for b, u0 in enumerate(range(0, N_TILES, CHUNK // n)):
+                per_bank = min(CHUNK // n, N_TILES - u0)
+                bank = psum.tile([P, per_bank, n], F32, name="bank", tag="bank%d" % banks[b])
                 res = stage.tile([P, per_bank, n], F32, name="res", tag="res")
                 for e in range(per_bank):
-                    u = b * per_bank + e
+                    u = u0 + e
                     nc.tensor.matmul_mx(
                         out=bank[:, e, :],
                         lhsT=wj_w[:, u * P : (u + 1) * P].bitcast(FP8X4),
@@ -226,7 +234,6 @@ def tile_list_transducer_joint_logits_kernel(
                         start=True,
                         stop=True,
                     )
-                u0 = b * per_bank
                 if b in on_vector:
                     nc.vector.tensor_tensor(
                         out=res[:],
@@ -247,12 +254,19 @@ def tile_list_transducer_joint_logits_kernel(
         join_tanh(0)
         join_gain(0)
         join_tanh(1)
-        logits(0, (0, 2))
-        join_gain(1)
         join_tanh(2)
-        logits(1, (1, 3))
+        logits(0, (0, 1), (7, 1, 2))
+        join_gain(1)
+        logits(1, (), (3, 7, 1))
+        coarse(0, 1, [3])
+        coarse(1, 1)
+        fine(0, 1)
+        fine(1, 1)
         join_gain(2)
         join_tanh(3)
-        logits(2, (1, 3))
+        logits(2, (0, 1, 2), (2, 3, 7, 1, 2))
         join_gain(3)
-        logits(3, (0, 2, 4))
+        join_tanh(4)
+        logits(3, (1, 4), (3, 7, 1, 2, 3))
+        join_gain(4)
+        logits(4, (0, 2, 4), (4, 5, 6, 0, 7))

@@ -20,7 +20,7 @@ ALU = mybir.AluOpType
 P = 128
 PASSES = 2
 CHUNK = 512
-PIECES = [(0, 128), (128, 128), (256, 256), (512, 256), (768, 256)]
+PIECES = [(0, 256), (256, 256), (512, 256), (768, 256)]
 N_TILES = N // P
 
 
@@ -73,8 +73,9 @@ def tile_list_transducer_joint_logits_kernel(
         nc.sync.dma_start(out=wc_raw[:], in_=wc_words.bitcast(I32).rearrange("a p c -> p a c"))
         load_scale_rows(wc_s_raw, wc_scales)
         tab_w = [load_table_words(0)]
-        for q in range(4):
-            nc.sync.dma_start(out=tab_s[32 * q : 32 * q + 8, :], in_=tab_scales.bitcast(I32)[:, 4 * q : 4 * q + 4, :])
+        tab_rows = tab_scales.bitcast(I32).rearrange("a (q r) c -> r q a c", r=4)
+        for r in range(4):
+            nc.sync.dma_start(out=tab_s[r:P:16, :], in_=tab_rows[r])
         wf_raw = [load_wf(0)]
         tab_w.append(load_table_words(1))
         wf_raw.append(load_wf(1))
@@ -92,7 +93,7 @@ def tile_list_transducer_joint_logits_kernel(
 
         def shift_scales():
             for r in range(4):
-                nc.sync.dma_start(out=v_s1[r:P:32, :], in_=v_s01[:].bitcast(I32)[4 + r : P : 32, :])
+                nc.sync.dma_start(out=v_s1[r:P:32, :], in_=v_s01[:].bitcast(I32)[16 + r : P : 32, :])
 
         def gather_words(a, c):
             if c == 1:
@@ -121,8 +122,8 @@ def tile_list_transducer_joint_logits_kernel(
 
         def cast_wf(copy, a, t0, t1):
             copy(
-                out=wf_bf[a][:, t0:t1, :, :].rearrange("p t m j -> p m t j"),
-                in_=wf_raw[a][:].rearrange("p j (m t) -> p m t j", t=4)[:, :, t0:t1, :],
+                out=wf_bf[a][:, t0:t1, :, :].rearrange("p t m j -> p m j t"),
+                in_=wf_raw[a][:].rearrange("p j (m t) -> p m j t", t=4)[:, :, :, t0:t1],
             )
 
         def quantize_wf(a, t0, t1):
@@ -134,10 +135,10 @@ def tile_list_transducer_joint_logits_kernel(
 
         acc = {}
 
-        def coarse(a, c, tiles=range(4)):
-            for t in tiles:
+        def coarse(a, c):
+            for t in range(4):
                 if a == 0:
-                    acc[c, t] = psum.tile([P, CHUNK], F32, name="acc", tag="bank%d" % ((4 * c + t) % 7))
+                    acc[c, t] = psum.tile([P, CHUNK], F32, name="acc", tag="bank%d" % (4 * c + t))
                 nc.tensor.matmul_mx(
                     out=acc[c, t][:],
                     lhsT=wc_w[:, a, t, :].bitcast(FP4X4),
@@ -189,11 +190,12 @@ def tile_list_transducer_joint_logits_kernel(
         quantize_wf(1, 2, 4)
         fine(1, 0)
         gather_words(0, 1)
-        coarse(0, 1, range(3))
+        coarse(0, 1)
         gather_words(1, 1)
 
         th = {}
-        hq = {}
+        h_w = held.tile([P, S], U32, name="h_w", align_bytes=64)
+        h_s = held.tile([P, S], U8, name="h_s", align_bytes=64)
 
         def join_tanh(i):
             j0, n = PIECES[i]
@@ -206,67 +208,69 @@ def tile_list_transducer_joint_logits_kernel(
             n = PIECES[i][1]
             hb = work.tile([P, n, 4], BF16, name="hb", tag="hb", align_bytes=64)
             nc.vector.tensor_tensor(
-                out=hb[:],
-                in0=th[i][:].rearrange("p t n -> p n t"),
-                in1=gain_sb[:].unsqueeze(1).to_broadcast([P, n, 4]),
+                out=hb[:].rearrange("p (c i) t -> p c t i", i=4),
+                in0=th[i][:].rearrange("p t (c i) -> p c t i", i=4),
+                in1=gain_sb[:].unsqueeze(1).unsqueeze(3).to_broadcast([P, n // 4, 4, 4]),
                 op=ALU.mult,
             )
-            h_w = held.tile([P, n], U32, name="h_w%d" % i, align_bytes=64)
-            h_s = held.tile([P, n], U8, name="h_s%d" % i, align_bytes=64)
-            nc.vector.quantize_mx(out=h_w[:].bitcast(FP8X4), scales=h_s[:], in_=hb[:].rearrange("p n t -> p (n t)"))
-            hq[i] = (h_w, h_s)
+            cols = slice(PIECES[i][0], PIECES[i][0] + n)
+            nc.vector.quantize_mx(
+                out=h_w[:, cols].bitcast(FP8X4), scales=h_s[:, cols], in_=hb[:].rearrange("p n t -> p (n t)")
+            )
 
-        def logits(i, on_vector, banks):
-            j0, n = PIECES[i]
-            h_w, h_s = hq[i]
-            for b, u0 in enumerate(range(0, N_TILES, CHUNK // n)):
-                per_bank = min(CHUNK // n, N_TILES - u0)
-                bank = psum.tile([P, per_bank, n], F32, name="bank", tag="bank%d" % banks[b])
-                res = stage.tile([P, per_bank, n], F32, name="res", tag="res")
-                for e in range(per_bank):
-                    u = u0 + e
-                    nc.tensor.matmul_mx(
-                        out=bank[:, e, :],
-                        lhsT=wj_w[:, u * P : (u + 1) * P].bitcast(FP8X4),
-                        lhsT_scale=wj_s[:].bitcast(U8)[:, u * P : (u + 1) * P],
-                        rhs=h_w[:].bitcast(FP8X4),
-                        rhs_scale=h_s[:],
-                        start=True,
-                        stop=True,
-                    )
-                if b in on_vector:
-                    nc.vector.tensor_tensor(
-                        out=res[:],
-                        in0=bank[:],
-                        in1=bias_sb[:, u0 : u0 + per_bank].unsqueeze(2).to_broadcast([P, per_bank, n]),
-                        op=ALU.add,
-                    )
-                else:
-                    for e in range(per_bank):
-                        nc.scalar.activation(
-                            res[:, e, :], bank[:, e, :], ACT.Identity, bias=bias_sb[:, u0 + e : u0 + e + 1]
-                        )
-                nc.sync.dma_start(
-                    out=out[u0 * P : (u0 + per_bank) * P, j0 : j0 + n].rearrange("(e p) j -> p e j", p=P),
-                    in_=res[:],
+        def logits_bank(res, u0, j0, n, engine, bank_no):
+            count = CHUNK // n
+            bank = psum.tile([P, count, n], F32, name="bank", tag="bank%d" % bank_no)
+            for e in range(count):
+                u = u0 + e
+                nc.tensor.matmul_mx(
+                    out=bank[:, e, :],
+                    lhsT=wj_w[:, u * P : (u + 1) * P].bitcast(FP8X4),
+                    lhsT_scale=wj_s[:].bitcast(U8)[:, u * P : (u + 1) * P],
+                    rhs=h_w[:, j0 : j0 + n].bitcast(FP8X4),
+                    rhs_scale=h_s[:, j0 : j0 + n],
+                    start=True,
+                    stop=True,
                 )
+            if engine == "V":
+                nc.vector.tensor_tensor(
+                    out=res,
+                    in0=bank[:],
+                    in1=bias_sb[:, u0 : u0 + count].unsqueeze(2).to_broadcast([P, count, n]),
+                    op=ALU.add,
+                )
+            else:
+                for e in range(count):
+                    nc.scalar.activation(res[:, e, :], bank[:, e, :], ACT.Identity, bias=bias_sb[:, u0 + e : u0 + e + 1])
+
+        def logits(u0, j0, n, engines, banks):
+            count = CHUNK // n
+            res = stage.tile([P, count * len(banks), n], F32, name="res", tag="res")
+            for b, bank_no in enumerate(banks):
+                logits_bank(res[:, b * count : (b + 1) * count, :], u0 + b * count, j0, n, engines[b], bank_no)
+            rows = slice(u0 * P, (u0 + count * len(banks)) * P)
+            nc.sync.dma_start(out=out[rows, j0 : j0 + n].rearrange("(e p) j -> p e j", p=P), in_=res[:])
 
         join_tanh(0)
         join_gain(0)
         join_tanh(1)
-        join_tanh(2)
-        logits(0, (0, 1), (7, 1, 2))
+        logits(0, 0, 256, "S", (0,))
         join_gain(1)
-        logits(1, (), (3, 7, 1))
-        coarse(0, 1, [3])
+        logits(2, 0, 256, "S", (1,))
         coarse(1, 1)
         fine(0, 1)
         fine(1, 1)
+        logits(4, 0, 512, "VS", (2, 3))
+        join_tanh(2)
+        logits(6, 0, 512, "VS", (0, 1))
         join_gain(2)
         join_tanh(3)
-        logits(2, (0, 1, 2), (2, 3, 7, 1, 2))
+        logits(8, 0, 512, "SV", (2, 3))
         join_gain(3)
-        join_tanh(4)
-        logits(3, (1, 4), (3, 7, 1, 2, 3))
-        join_gain(4)
-        logits(4, (0, 2, 4), (4, 5, 6, 0, 7))
+        logits(0, 256, 256, "SS", (0, 1))
+        logits(0, 512, 512, "VS", (4, 5))
+        logits(2, 512, 512, "VS", (6, 7))
+        logits(4, 512, 512, "VS", (2, 3))
+        logits(6, 512, 512, "VS", (0, 1))
+        logits(8, 512, 512, "V", (4,))
+        logits(9, 512, 512, "S", (5,))

@@ -267,10 +267,9 @@ def tile_list_transducer_joint_logits_kernel(
         join_tanh(3)
         logits(8, 0, 512, "SV", (2, 3))
         join_gain(3)
-        logits(0, 256, 256, "SS", (0, 1))
-        logits(0, 512, 512, "VS", (4, 5))
-        logits(2, 512, 512, "VS", (6, 7))
-        logits(4, 512, 512, "VS", (2, 3))
-        logits(6, 512, 512, "VS", (0, 1))
-        logits(8, 512, 512, "V", (4,))
-        logits(9, 512, 512, "S", (5,))
+        logits(0, 256, 512, "SS", (0, 1))
+        logits(2, 256, 512, "SV", (2, 3))
+        logits(4, 512, 512, "VS", (4, 5))
+        logits(6, 512, 512, "VS", (6, 7))
+        logits(8, 512, 512, "VS", (0, 1))
+        logits(0, 768, 256, "VS", (2, 3))

@@ -1,7 +1,6 @@
 from contextlib import ExitStack
 
 import concourse.mybir as mybir
-from concourse.masks import make_identity
 
 K, H, N, T, S = 1024, 512, 1280, 2048, 1024
 FLOPS = 2 * S * (2 * K * H + H * N)
@@ -22,6 +21,7 @@ PASSES = 2
 CHUNK = 512
 PIECES = [(0, 256), (256, 256), (512, 256), (768, 256)]
 N_TILES = N // P
+CAST_SPLIT = (32, 88)
 
 
 def tile_list_transducer_joint_logits_kernel(
@@ -31,26 +31,25 @@ def tile_list_transducer_joint_logits_kernel(
     with ExitStack() as ctx:
         held = ctx.enter_context(tc.tile_pool(name="held", bufs=1))
         work = ctx.enter_context(tc.tile_pool(name="work", bufs=3))
-        stage = ctx.enter_context(tc.tile_pool(name="stage", bufs=10))
+        stage = ctx.enter_context(tc.tile_pool(name="stage", bufs=14))
         psum = ctx.enter_context(tc.psum_pool(name="psum", bufs=1))
 
-        offsets = held.tile([P, S // 16], U16, name="offsets")
         ring = ctx.enter_context(tc.tile_pool(name="ring", bufs=1))
-        tab_s = ring.tile([P, T // 4], I32, name="tab_s", align_bytes=64, offset=16384)
-        wc_s_raw = held.tile([P, PASSES * H // 4], I32, name="wc_s_raw", align_bytes=64)
-        wj_s = held.tile([P, N // 4], I32, name="wj_s", align_bytes=64)
+
+        WF_BF1, GAIN, BIAS, WF1 = 0, 4096, 4128, 4224
+        TAB_S = GAIN
+        TAB0 = WF1 + 8192
+        V_W10 = TAB0 + 8192
+        WC_S_RAW = V_W10 + 4096
+        offsets = held.tile([P, S // 16], U16, name="offsets")
+        tab_s = ring.tile([P, T // 4], I32, name="tab_s", align_bytes=64, offset=TAB_S)
+        wc_s_raw = ring.tile([P, PASSES * H // 4], I32, name="wc_s_raw", align_bytes=64, offset=WC_S_RAW)
         warm = held.tile([P, 2], F32, name="warm")
         v_s1 = held.tile([P, S // 4], I32, name="v_s1", align_bytes=64)
-        ident = held.tile([P, P], F32, name="ident")
-        bias_rows = held.tile([P, P], F32, name="bias_rows")
-        nc.gpsimd.memset(bias_rows[:], 0.0)
-        nc.scalar.dma_start(out=bias_rows[0:N_TILES, :], in_=bias.rearrange("(u p) -> u p", p=P))
-        nc.gpsimd.memset(wc_s_raw[:], 0)
-        nc.vector.memset(tab_s[:], 0)
-        nc.vector.memset(v_s1[:], 0)
-        nc.vector.memset(wj_s[:], 0)
+        nc.gpsimd.memset(tab_s[:], 0)
         nc.vector.memset(warm[:, 0:1], 0.0)
-        make_identity(nc, ident[:])
+        nc.vector.memset(wc_s_raw[:], 0)
+        nc.vector.memset(v_s1[:], 0)
         nc.scalar.activation(warm[:, 1:2], warm[:, 0:1], ACT.Tanh)
 
         def load_scale_rows(dst, src):
@@ -58,139 +57,139 @@ def tile_list_transducer_joint_logits_kernel(
             for r in range(4):
                 nc.sync.dma_start(out=dst[r:P:32, :].rearrange("q (a c) -> q a c", a=src.shape[0]), in_=rows[r])
 
-        def load_table_words(a):
-            t_w = held.tile([P, T], I32, name="tab_w%d" % a, align_bytes=64)
+        def load_table_words(t_w, a):
             nc.sync.dma_start(out=t_w[:], in_=tab_words[a].rearrange("p t i -> p (t i)").bitcast(I32))
-            return t_w
 
         def load_wf(a):
-            w = ring.tile([P, 4, H], F32, name="wf_raw%d" % a, align_bytes=64, offset=8192 * a)
+            if a == 0:
+                w = held.tile([P, 4, H], F32, name="wf_raw0", align_bytes=64)
+            else:
+                w = ring.tile([P, 4, H], F32, name="wf_raw1", align_bytes=64, offset=WF1)
             nc.sync.dma_start(out=w[:], in_=wf[512 * a : 512 * (a + 1), :].rearrange("(p j) c -> p j c", j=4))
             return w
 
         nc.sync.dma_start(offsets[:], offs)
-        wc_raw = held.tile([P, PASSES, H // 2], I32, name="wc_raw", align_bytes=64)
-        nc.sync.dma_start(out=wc_raw[:], in_=wc_words.bitcast(I32).rearrange("a p c -> p a c"))
-        load_scale_rows(wc_s_raw, wc_scales)
-        tab_w = [load_table_words(0)]
+        enc_sb = held.tile([P, 4], F32, name="enc_sb")
+        nc.sync.dma_start(out=enc_sb[:], in_=enc.rearrange("(p t) -> p t", t=4))
         tab_rows = tab_scales.bitcast(I32).rearrange("a (q r) c -> r q a c", r=4)
         for r in range(4):
             nc.sync.dma_start(out=tab_s[r:P:16, :], in_=tab_rows[r])
+        tab_w0 = ring.tile([P, T], I32, name="tab_w0", align_bytes=64, offset=TAB0)
+        tab_w1 = held.tile([P, T], I32, name="tab_w1", align_bytes=64)
+        tab_w = [tab_w0, tab_w1]
+        load_table_words(tab_w[0], 0)
+        wc_raw = held.tile([P, PASSES, H // 2], I32, name="wc_raw", align_bytes=64)
+        nc.sync.dma_start(out=wc_raw[:], in_=wc_words.bitcast(I32).rearrange("a p c -> p a c"))
+        load_scale_rows(wc_s_raw, wc_scales)
         wf_raw = [load_wf(0)]
-        tab_w.append(load_table_words(1))
-        wf_raw.append(load_wf(1))
+        load_table_words(tab_w[1], 1)
 
-        v_s = {}
         v_w = {}
-
         v_s01 = held.tile([P, S], U8, name="v_s01", align_bytes=64)
+        v_s = {}
+        for c in range(2):
+            v_s[0, c] = v_s01[:, c * CHUNK : (c + 1) * CHUNK]
+            v_s[1, c] = v_s1[:].bitcast(U8)[:, c * CHUNK : (c + 1) * CHUNK]
 
-        def gather_scales(c):
-            cols = slice(c * CHUNK, (c + 1) * CHUNK)
-            nc.vector.tensor_copy(v_s01[:, cols], tab_s[:].bitcast(U8).indirect(offsets[:, 32 * c : 32 * (c + 1)]))
-            v_s[0, c] = v_s01[:, cols]
-            v_s[1, c] = v_s1[:].bitcast(U8)[:, cols]
-
-        def shift_scales():
+        def gather_scales():
+            nc.vector.tensor_copy(v_s01[:], tab_s[:].bitcast(U8).indirect(offsets[:]))
             for r in range(4):
                 nc.sync.dma_start(out=v_s1[r:P:32, :], in_=v_s01[:].bitcast(I32)[16 + r : P : 32, :])
 
         def gather_words(a, c):
             if c == 1:
-                g = ring.tile([P, CHUNK], U32, name="v_w%d1" % a, align_bytes=64, offset=(16384, 8192)[a])
+                g = ring.tile([P, CHUNK], U32, name="v_w%d1" % a, align_bytes=64, offset=(WC_S_RAW, WF_BF1)[a])
+            elif (a, c) == (1, 0):
+                g = ring.tile([P, CHUNK], U32, name="v_w10", align_bytes=64, offset=V_W10)
             else:
-                g = held.tile([P, CHUNK], U32, name="v_w%d0" % a, align_bytes=64)
+                g = held.tile([P, CHUNK], U32, name="v_w%d%d" % (a, c), align_bytes=64)
             nc.vector.tensor_copy(g[:], tab_w[a][:].bitcast(U32).indirect(offsets[:, 32 * c : 32 * (c + 1)]))
             v_w[a, c] = g
 
         wc_w = held.tile([P, PASSES, 4, 2 * P], U8, name="wc_w", align_bytes=64)
         wc_s = held.tile([P, PASSES, 4, P], U8, name="wc_s", align_bytes=64)
 
-        def permute_wc(a):
+        def permute_wc_words():
             nc.vector.tensor_copy(
-                out=wc_w[:, a, :, :].bitcast(U16),
-                in_=wc_raw[:, a, :].bitcast(U16).rearrange("p (m t) -> p t m", t=4),
-            )
-            nc.vector.tensor_copy(
-                out=wc_s[:, a, :, :],
-                in_=wc_s_raw[:].bitcast(U8)[:, a * H : (a + 1) * H].rearrange("p (m t) -> p t m", t=4),
+                out=wc_w[:].bitcast(U16),
+                in_=wc_raw[:].bitcast(U16).rearrange("p a (m t) -> p a t m", t=4),
             )
 
-        wf_bf = [held.tile([P, 4, P, 4], BF16, name="wf_bf%d" % a, align_bytes=64) for a in range(PASSES)]
-        wf_w = held.tile([P, PASSES, 4, P], U32, name="wf_w", align_bytes=64)
-        wf_s = held.tile([P, PASSES, 4, P], U8, name="wf_s", align_bytes=64)
-
-        def cast_wf(copy, a, t0, t1):
-            copy(
-                out=wf_bf[a][:, t0:t1, :, :].rearrange("p t m j -> p m j t"),
-                in_=wf_raw[a][:].rearrange("p j (m t) -> p m j t", t=4)[:, :, :, t0:t1],
+        def permute_wc_scales():
+            nc.vector.tensor_copy(
+                out=wc_s[:],
+                in_=wc_s_raw[:].bitcast(U8).rearrange("p (a m t) -> p a t m", a=PASSES, t=4),
             )
+
+        wf_bf0 = held.tile([P, 4, P, 4], BF16, name="wf_bf0", align_bytes=64)
+        wf_bf1 = ring.tile([P, 4, P, 4], BF16, name="wf_bf1", align_bytes=64, offset=WF_BF1)
+        wf_bf = [wf_bf0, wf_bf1]
+        wf_w = [held.tile([P, 4, P], U32, name="wf_w%d" % a, align_bytes=64) for a in range(PASSES)]
+        wf_s = [held.tile([P, 4, P], U8, name="wf_s%d" % a, align_bytes=64) for a in range(PASSES)]
+
+        def cast_wf(a):
+            for copy, m0, m1 in ((nc.vector.tensor_copy, 0, CAST_SPLIT[a]), (nc.scalar.copy, CAST_SPLIT[a], P)):
+                copy(
+                    out=wf_bf[a][:, :, m0:m1, :].rearrange("p t m j -> p m j t"),
+                    in_=wf_raw[a][:].rearrange("p j (m t) -> p m j t", t=4)[:, m0:m1, :, :],
+                )
 
         def quantize_wf(a, t0, t1):
             nc.vector.quantize_mx(
-                out=wf_w[:, a, t0:t1, :].rearrange("p t m -> p (t m)").bitcast(FP8X4),
-                scales=wf_s[:, a, t0:t1, :].rearrange("p t m -> p (t m)"),
+                out=wf_w[a][:, t0:t1, :].rearrange("p t m -> p (t m)").bitcast(FP8X4),
+                scales=wf_s[a][:, t0:t1, :].rearrange("p t m -> p (t m)"),
                 in_=wf_bf[a][:, t0:t1, :, :].rearrange("p t m j -> p (t m j)"),
             )
 
         acc = {}
 
-        def coarse(a, c):
+        def stage1(kind, a, c, start=False, stop=False):
             for t in range(4):
-                if a == 0:
+                if start:
                     acc[c, t] = psum.tile([P, CHUNK], F32, name="acc", tag="bank%d" % (4 * c + t))
+                if kind == "coarse":
+                    lhsT, lhsT_scale = wc_w[:, a, t, :].bitcast(FP4X4), wc_s[:, a, t, :]
+                else:
+                    lhsT, lhsT_scale = wf_w[a][:, t, :].bitcast(FP8X4), wf_s[a][:, t, :]
                 nc.tensor.matmul_mx(
                     out=acc[c, t][:],
-                    lhsT=wc_w[:, a, t, :].bitcast(FP4X4),
-                    lhsT_scale=wc_s[:, a, t, :],
+                    lhsT=lhsT,
+                    lhsT_scale=lhsT_scale,
                     rhs=v_w[a, c][:].bitcast(FP8X4),
                     rhs_scale=v_s[a, c],
-                    start=(a == 0),
-                    stop=False,
+                    start=start,
+                    stop=stop,
                 )
 
-        def fine(a, c):
-            for t in range(4):
-                nc.tensor.matmul_mx(
-                    out=acc[c, t][:],
-                    lhsT=wf_w[:, a, t, :].bitcast(FP8X4),
-                    lhsT_scale=wf_s[:, a, t, :],
-                    rhs=v_w[a, c][:].bitcast(FP8X4),
-                    rhs_scale=v_s[a, c],
-                    start=False,
-                    stop=(a == PASSES - 1),
-                )
-
-        permute_wc(0)
-        permute_wc(1)
-        bias_ps = psum.tile([P, P], F32, name="bias_ps", tag="bank7")
-        nc.tensor.transpose(bias_ps[:], bias_rows[:], ident[:])
-        bias_sb = held.tile([P, N_TILES], F32, name="bias_sb")
-        nc.scalar.copy(out=bias_sb[:], in_=bias_ps[:, 0:N_TILES])
-        gather_words(0, 0)
-        gather_scales(0)
-        gather_scales(1)
-        shift_scales()
-        enc_sb = held.tile([P, 4], F32, name="enc_sb")
-        gain_sb = held.tile([P, 4], F32, name="gain_sb")
-        nc.sync.dma_start(out=enc_sb[:], in_=enc.rearrange("(p t) -> p t", t=4))
+        gather_scales()
+        wf_raw.append(load_wf(1))
+        gain_sb = ring.tile([P, 4], F32, name="gain_sb", offset=GAIN)
         nc.sync.dma_start(out=gain_sb[:], in_=gain.rearrange("(p t) -> p t", t=4))
-        wj_w = held.tile([P, N], I32, name="wj_w", align_bytes=64)
-        nc.sync.dma_start(out=wj_w[:], in_=wj_words[0].rearrange("p c i -> p (c i)").bitcast(I32))
-        load_scale_rows(wj_s, wj_scales)
-        coarse(0, 0)
-        cast_wf(nc.scalar.copy, 0, 0, 4)
-        quantize_wf(0, 0, 4)
-        fine(0, 0)
-        gather_words(1, 0)
-        coarse(1, 0)
-        cast_wf(nc.vector.tensor_copy, 1, 0, 2)
-        cast_wf(nc.scalar.copy, 1, 2, 4)
-        quantize_wf(1, 0, 2)
-        quantize_wf(1, 2, 4)
-        fine(1, 0)
+        gather_words(0, 0)
+        permute_wc_words()
+        permute_wc_scales()
+        stage1("coarse", 0, 0, start=True)
         gather_words(0, 1)
-        coarse(0, 1)
+        stage1("coarse", 0, 1, start=True)
+        wj_w = ring.tile([P, N], I32, name="wj_w", align_bytes=64, offset=TAB0)
+        wj_s = ring.tile([P, N // 4], I32, name="wj_s", align_bytes=64, offset=TAB0 + 4 * N)
+        bias_sb = ring.tile([P, N_TILES], F32, name="bias_sb", offset=BIAS)
+        nc.sync.dma_start(out=wj_w[:], in_=wj_words[0].rearrange("p c i -> p (c i)").bitcast(I32))
+        nc.vector.memset(wj_s[:], 0)
+        load_scale_rows(wj_s, wj_scales)
+        with nc.allow_non_contiguous_dma(reason="one bias value for each partition and output tile"):
+            nc.sync.dma_start(out=bias_sb[:], in_=bias.rearrange("(u p) -> p u", p=P))
+        cast_wf(0)
+        quantize_wf(0, 0, 4)
+        gather_words(1, 0)
+        stage1("fine", 0, 0)
+        stage1("fine", 0, 1)
+        stage1("coarse", 1, 0)
+        cast_wf(1)
+        quantize_wf(1, 0, 1)
+        quantize_wf(1, 1, 2)
+        quantize_wf(1, 2, 4)
+        stage1("fine", 1, 0, stop=True)
         gather_words(1, 1)
 
         th = {}
@@ -200,13 +199,16 @@ def tile_list_transducer_joint_logits_kernel(
         def join_tanh(i):
             j0, n = PIECES[i]
             c, o = divmod(j0, CHUNK)
-            th[i] = work.tile([P, 4, n], F32, name="th", tag="th", align_bytes=64)
+            if i == 1:
+                th[i] = ring.tile([P, 4, n], F32, name="th1", align_bytes=64, offset=V_W10)
+            else:
+                th[i] = work.tile([P, 4, n], F32, name="th", tag="th%d" % (i // 2), bufs=1, align_bytes=64)
             for t in range(4):
                 nc.scalar.activation(th[i][:, t, :], acc[c, t][:, o : o + n], ACT.Tanh, bias=enc_sb[:, t : t + 1])
 
         def join_gain(i):
             n = PIECES[i][1]
-            hb = work.tile([P, n, 4], BF16, name="hb", tag="hb", align_bytes=64)
+            hb = work.tile([P, n, 4], BF16, name="hb", tag="hb%d" % (i // 3), bufs=1, align_bytes=64)
             nc.vector.tensor_tensor(
                 out=hb[:].rearrange("p (c i) t -> p c t i", i=4),
                 in0=th[i][:].rearrange("p t (c i) -> p c t i", i=4),
@@ -243,11 +245,14 @@ def tile_list_transducer_joint_logits_kernel(
                 for e in range(count):
                     nc.scalar.activation(res[:, e, :], bank[:, e, :], ACT.Identity, bias=bias_sb[:, u0 + e : u0 + e + 1])
 
+        res_of = {}
+
         def logits(u0, j0, n, engines, banks):
             count = CHUNK // n
             res = stage.tile([P, count * len(banks), n], F32, name="res", tag="res")
             for b, bank_no in enumerate(banks):
                 logits_bank(res[:, b * count : (b + 1) * count, :], u0 + b * count, j0, n, engines[b], bank_no)
+            res_of[u0, j0] = res
             rows = slice(u0 * P, (u0 + count * len(banks)) * P)
             nc.sync.dma_start(out=out[rows, j0 : j0 + n].rearrange("(e p) j -> p e j", p=P), in_=res[:])
 
@@ -255,21 +260,24 @@ def tile_list_transducer_joint_logits_kernel(
         join_gain(0)
         join_tanh(1)
         logits(0, 0, 256, "S", (0,))
-        join_gain(1)
         logits(2, 0, 256, "S", (1,))
-        coarse(1, 1)
-        fine(0, 1)
-        fine(1, 1)
-        logits(4, 0, 512, "VS", (2, 3))
+        logits(4, 0, 256, "S", (2,))
+        join_gain(1)
+        stage1("coarse", 1, 1)
+        stage1("fine", 1, 1, stop=True)
         join_tanh(2)
-        logits(6, 0, 512, "VS", (0, 1))
+        logits(6, 0, 512, "S", (3,))
+        logits(7, 0, 512, "S", (0,))
         join_gain(2)
         join_tanh(3)
-        logits(8, 0, 512, "SV", (2, 3))
+        logits(8, 0, 512, "V", (1,))
+        logits(9, 0, 512, "V", (2,))
+        logits(0, 256, 512, "V", (3,))
+        logits(1, 256, 512, "V", (0,))
         join_gain(3)
-        logits(0, 256, 512, "SS", (0, 1))
-        logits(2, 256, 512, "SV", (2, 3))
-        logits(4, 512, 512, "VS", (4, 5))
+        logits(2, 256, 512, "SS", (1, 2))
+        logits(4, 256, 512, "SS", (3, 0))
+        logits(0, 768, 256, "VS", (4, 5))
         logits(6, 512, 512, "VS", (6, 7))
-        logits(8, 512, 512, "VS", (0, 1))
-        logits(0, 768, 256, "VS", (2, 3))
+        logits(4, 768, 256, "V", (1,))
+        logits(8, 512, 512, "SV", (2, 3))

@@ -1,6 +1,7 @@
 from contextlib import ExitStack
 
 import concourse.mybir as mybir
+from concourse.masks import make_identity
 
 K, H, N, T, S = 1024, 512, 1280, 2048, 1024
 FLOPS = 2 * S * (2 * K * H + H * N)
@@ -31,12 +32,11 @@ def tile_list_transducer_joint_logits_kernel(
     with ExitStack() as ctx:
         held = ctx.enter_context(tc.tile_pool(name="held", bufs=1))
         work = ctx.enter_context(tc.tile_pool(name="work", bufs=3))
-        stage = ctx.enter_context(tc.tile_pool(name="stage", bufs=14))
         psum = ctx.enter_context(tc.psum_pool(name="psum", bufs=1))
 
         ring = ctx.enter_context(tc.tile_pool(name="ring", bufs=1))
 
-        WF_BF1, GAIN, BIAS, WF1 = 0, 4096, 4128, 4224
+        WF_BF1, GAIN, WF1 = 0, 4096, 4160
         TAB_S = GAIN
         TAB0 = WF1 + 8192
         V_W10 = TAB0 + 8192
@@ -46,7 +46,12 @@ def tile_list_transducer_joint_logits_kernel(
         wc_s_raw = ring.tile([P, PASSES * H // 4], I32, name="wc_s_raw", align_bytes=64, offset=WC_S_RAW)
         warm = held.tile([P, 2], F32, name="warm")
         v_s1 = held.tile([P, S // 4], I32, name="v_s1", align_bytes=64)
+        ident = held.tile([P, P], F32, name="ident")
+        bias_rows = held.tile([P, P], F32, name="bias_rows")
         nc.gpsimd.memset(tab_s[:], 0)
+        nc.gpsimd.memset(bias_rows[:], 0.0)
+        nc.gpsimd.dma_start(out=bias_rows[0:N_TILES, :], in_=bias.rearrange("(u p) -> u p", p=P))
+        make_identity(nc, ident[:])
         nc.vector.memset(warm[:, 0:1], 0.0)
         nc.vector.memset(wc_s_raw[:], 0)
         nc.vector.memset(v_s1[:], 0)
@@ -161,6 +166,10 @@ def tile_list_transducer_joint_logits_kernel(
                     stop=stop,
                 )
 
+        bias_ps = psum.tile([P, P], F32, name="bias_ps", tag="bank7")
+        nc.tensor.transpose(bias_ps[:], bias_rows[:], ident[:])
+        bias_sb = held.tile([P, N_TILES], F32, name="bias_sb")
+        nc.scalar.copy(out=bias_sb[:], in_=bias_ps[:, 0:N_TILES])
         gather_scales()
         wf_raw.append(load_wf(1))
         gain_sb = ring.tile([P, 4], F32, name="gain_sb", offset=GAIN)
@@ -173,12 +182,9 @@ def tile_list_transducer_joint_logits_kernel(
         stage1("coarse", 0, 1, start=True)
         wj_w = ring.tile([P, N], I32, name="wj_w", align_bytes=64, offset=TAB0)
         wj_s = ring.tile([P, N // 4], I32, name="wj_s", align_bytes=64, offset=TAB0 + 4 * N)
-        bias_sb = ring.tile([P, N_TILES], F32, name="bias_sb", offset=BIAS)
         nc.sync.dma_start(out=wj_w[:], in_=wj_words[0].rearrange("p c i -> p (c i)").bitcast(I32))
         nc.vector.memset(wj_s[:], 0)
         load_scale_rows(wj_s, wj_scales)
-        with nc.allow_non_contiguous_dma(reason="one bias value for each partition and output tile"):
-            nc.sync.dma_start(out=bias_sb[:], in_=bias.rearrange("(u p) -> p u", p=P))
         cast_wf(0)
         quantize_wf(0, 0, 4)
         gather_words(1, 0)
@@ -199,10 +205,10 @@ def tile_list_transducer_joint_logits_kernel(
         def join_tanh(i):
             j0, n = PIECES[i]
             c, o = divmod(j0, CHUNK)
-            if i == 1:
-                th[i] = ring.tile([P, 4, n], F32, name="th1", align_bytes=64, offset=V_W10)
+            if i % 2:
+                th[i] = ring.tile([P, 4, n], F32, name="th%d" % i, align_bytes=64, offset=V_W10)
             else:
-                th[i] = work.tile([P, 4, n], F32, name="th", tag="th%d" % (i // 2), bufs=1, align_bytes=64)
+                th[i] = work.tile([P, 4, n], F32, name="th", tag="th%d" % i, bufs=1, align_bytes=64)
             for t in range(4):
                 nc.scalar.activation(th[i][:, t, :], acc[c, t][:, o : o + n], ACT.Tanh, bias=enc_sb[:, t : t + 1])
 
@@ -220,8 +226,14 @@ def tile_list_transducer_joint_logits_kernel(
                 out=h_w[:, cols].bitcast(FP8X4), scales=h_s[:, cols], in_=hb[:].rearrange("p n t -> p (n t)")
             )
 
-        def logits_bank(res, u0, j0, n, engine, bank_no):
-            count = CHUNK // n
+        res_of = {}
+
+        def open_store(u0, count, j0, n):
+            res_of[u0, j0] = held.tile([P, count, n], F32, name="res%d_%d" % (u0, j0))
+
+        def logits(store, u0, count, j0, engine, bank_no):
+            n = CHUNK // count
+            res = res_of[store][:, u0 - store[0] : u0 - store[0] + count, j0 - store[1] : j0 - store[1] + n]
             bank = psum.tile([P, count, n], F32, name="bank", tag="bank%d" % bank_no)
             for e in range(count):
                 u = u0 + e
@@ -245,39 +257,46 @@ def tile_list_transducer_joint_logits_kernel(
                 for e in range(count):
                     nc.scalar.activation(res[:, e, :], bank[:, e, :], ACT.Identity, bias=bias_sb[:, u0 + e : u0 + e + 1])
 
-        res_of = {}
-
-        def logits(u0, j0, n, engines, banks):
-            count = CHUNK // n
-            res = stage.tile([P, count * len(banks), n], F32, name="res", tag="res")
-            for b, bank_no in enumerate(banks):
-                logits_bank(res[:, b * count : (b + 1) * count, :], u0 + b * count, j0, n, engines[b], bank_no)
-            res_of[u0, j0] = res
-            rows = slice(u0 * P, (u0 + count * len(banks)) * P)
+        def close_store(u0, j0):
+            res = res_of[u0, j0]
+            count, n = res.shape[1], res.shape[2]
+            rows = slice(u0 * P, (u0 + count) * P)
             nc.sync.dma_start(out=out[rows, j0 : j0 + n].rearrange("(e p) j -> p e j", p=P), in_=res[:])
+
+        def one_bank_store(u0, count, j0, engine, bank_no):
+            open_store(u0, count, j0, CHUNK // count)
+            logits((u0, j0), u0, count, j0, engine, bank_no)
+            close_store(u0, j0)
 
         join_tanh(0)
         join_gain(0)
         join_tanh(1)
-        logits(0, 0, 256, "S", (0,))
-        logits(2, 0, 256, "S", (1,))
-        logits(4, 0, 256, "S", (2,))
+        one_bank_store(0, 2, 0, "S", 0)
+        one_bank_store(2, 2, 0, "S", 1)
         join_gain(1)
         stage1("coarse", 1, 1)
         stage1("fine", 1, 1, stop=True)
         join_tanh(2)
-        logits(6, 0, 512, "S", (3,))
-        logits(7, 0, 512, "S", (0,))
         join_gain(2)
+        one_bank_store(4, 1, 0, "S", 2)
         join_tanh(3)
-        logits(8, 0, 512, "V", (1,))
-        logits(9, 0, 512, "V", (2,))
-        logits(0, 256, 512, "V", (3,))
-        logits(1, 256, 512, "V", (0,))
         join_gain(3)
-        logits(2, 256, 512, "SS", (1, 2))
-        logits(4, 256, 512, "SS", (3, 0))
-        logits(0, 768, 256, "VS", (4, 5))
-        logits(6, 512, 512, "VS", (6, 7))
-        logits(4, 768, 256, "V", (1,))
-        logits(8, 512, 512, "SV", (2, 3))
+        one_bank_store(5, 1, 0, "S", 3)
+        one_bank_store(6, 1, 0, "S", 0)
+        one_bank_store(7, 1, 0, "S", 1)
+        for u in (8, 9):
+            open_store(u, 1, 0, 1024)
+            logits((u, 0), u, 1, 0, "S", u - 6)
+            logits((u, 0), u, 1, 512, "V", u - 4)
+            close_store(u, 0)
+        for u in (0, 2):
+            open_store(u, 2, 256, 768)
+            logits((u, 256), u, 1, 256, "S", u)
+            logits((u, 256), u + 1, 1, 256, "V", u + 1)
+            logits((u, 256), u, 2, 768, "V", 6 + u // 2)
+            close_store(u, 256)
+        for u in (4, 6):
+            open_store(u, 2, 512, 512)
+            logits((u, 512), u, 1, 512, "S", u)
+            logits((u, 512), u + 1, 1, 512, "V", u + 1)
+            close_store(u, 512)

@@ -41,6 +41,9 @@ def tile_list_transducer_joint_logits_kernel(
         TAB0 = WF1 + 8192
         V_W10 = TAB0 + 8192
         WC_S_RAW = V_W10 + 4096
+        HB1 = WC_S_RAW + 2048
+        HB0 = HB1 + 1024
+        TH3 = HB0 + 1024
         offsets = held.tile([P, S // 16], U16, name="offsets")
         tab_s = ring.tile([P, T // 4], I32, name="tab_s", align_bytes=64, offset=TAB_S)
         wc_s_raw = ring.tile([P, PASSES * H // 4], I32, name="wc_s_raw", align_bytes=64, offset=WC_S_RAW)
@@ -206,7 +209,7 @@ def tile_list_transducer_joint_logits_kernel(
             j0, n = PIECES[i]
             c, o = divmod(j0, CHUNK)
             if i % 2:
-                th[i] = ring.tile([P, 4, n], F32, name="th%d" % i, align_bytes=64, offset=V_W10)
+                th[i] = ring.tile([P, 4, n], F32, name="th%d" % i, align_bytes=64, offset=(V_W10, TH3)[i // 2])
             else:
                 th[i] = work.tile([P, 4, n], F32, name="th", tag="th%d" % i, bufs=1, align_bytes=64)
             for t in range(4):
@@ -214,7 +217,10 @@ def tile_list_transducer_joint_logits_kernel(
 
         def join_gain(i):
             n = PIECES[i][1]
-            hb = work.tile([P, n, 4], BF16, name="hb", tag="hb%d" % (i // 3), bufs=1, align_bytes=64)
+            if i < 2:
+                hb = ring.tile([P, n, 4], BF16, name="hb%d" % i, align_bytes=64, offset=(HB0, HB1)[i])
+            else:
+                hb = held.tile([P, n, 4], BF16, name="hb%d" % i, align_bytes=64)
             nc.vector.tensor_tensor(
                 out=hb[:].rearrange("p (c i) t -> p c t i", i=4),
                 in0=th[i][:].rearrange("p t (c i) -> p c t i", i=4),
@@ -272,18 +278,16 @@ def tile_list_transducer_joint_logits_kernel(
         join_gain(0)
         join_tanh(1)
         one_bank_store(0, 2, 0, "S", 0)
-        one_bank_store(2, 2, 0, "S", 1)
         join_gain(1)
         stage1("coarse", 1, 1)
         stage1("fine", 1, 1, stop=True)
         join_tanh(2)
         join_gain(2)
-        one_bank_store(4, 1, 0, "S", 2)
         join_tanh(3)
         join_gain(3)
-        one_bank_store(5, 1, 0, "S", 3)
-        one_bank_store(6, 1, 0, "S", 0)
-        one_bank_store(7, 1, 0, "S", 1)
+        one_bank_store(2, 2, 0, "S", 1)
+        for u in range(4, 8):
+            one_bank_store(u, 1, 0, "S", (u + 2) % 4)
         for u in (8, 9):
             open_store(u, 1, 0, 1024)
             logits((u, 0), u, 1, 0, "S", u - 6)
@@ -292,11 +296,11 @@ def tile_list_transducer_joint_logits_kernel(
         for u in (0, 2):
             open_store(u, 2, 256, 768)
             logits((u, 256), u, 1, 256, "S", u)
-            logits((u, 256), u + 1, 1, 256, "V", u + 1)
+            logits((u, 256), u + 1, 1, 256, "S", u + 1)
             logits((u, 256), u, 2, 768, "V", 6 + u // 2)
             close_store(u, 256)
         for u in (4, 6):
             open_store(u, 2, 512, 512)
-            logits((u, 512), u, 1, 512, "S", u)
+            logits((u, 512), u, 1, 512, "V", u)
             logits((u, 512), u + 1, 1, 512, "V", u + 1)
             close_store(u, 512)

@@ -1,7 +1,6 @@
 from contextlib import ExitStack
 
 import concourse.mybir as mybir
-from concourse.masks import make_identity
 
 K, H, N, T, S = 1024, 512, 1280, 2048, 1024
 FLOPS = 2 * S * (2 * K * H + H * N)
@@ -49,12 +48,7 @@ def tile_list_transducer_joint_logits_kernel(
         wc_s_raw = ring.tile([P, PASSES * H // 4], I32, name="wc_s_raw", align_bytes=64, offset=WC_S_RAW)
         warm = held.tile([P, 2], F32, name="warm")
         v_s1 = held.tile([P, S // 4], I32, name="v_s1", align_bytes=64)
-        ident = held.tile([P, P], F32, name="ident")
-        bias_rows = held.tile([P, P], F32, name="bias_rows")
         nc.gpsimd.memset(tab_s[:], 0)
-        nc.gpsimd.memset(bias_rows[:], 0.0)
-        nc.gpsimd.dma_start(out=bias_rows[0:N_TILES, :], in_=bias.rearrange("(u p) -> u p", p=P))
-        make_identity(nc, ident[:])
         nc.vector.memset(warm[:, 0:1], 0.0)
         nc.vector.memset(wc_s_raw[:], 0)
         nc.vector.memset(v_s1[:], 0)
@@ -169,10 +163,6 @@ def tile_list_transducer_joint_logits_kernel(
                     stop=stop,
                 )
 
-        bias_ps = psum.tile([P, P], F32, name="bias_ps", tag="bank7")
-        nc.tensor.transpose(bias_ps[:], bias_rows[:], ident[:])
-        bias_sb = held.tile([P, N_TILES], F32, name="bias_sb")
-        nc.scalar.copy(out=bias_sb[:], in_=bias_ps[:, 0:N_TILES])
         gather_scales()
         wf_raw.append(load_wf(1))
         gain_sb = ring.tile([P, 4], F32, name="gain_sb", offset=GAIN)
@@ -188,8 +178,12 @@ def tile_list_transducer_joint_logits_kernel(
         nc.sync.dma_start(out=wj_w[:], in_=wj_words[0].rearrange("p c i -> p (c i)").bitcast(I32))
         nc.vector.memset(wj_s[:], 0)
         load_scale_rows(wj_s, wj_scales)
+        bias_sb = held.tile([P, N_TILES], F32, name="bias_sb")
+        with nc.allow_non_contiguous_dma(reason="one bias value for each partition and output tile"):
+            nc.sync.dma_start(out=bias_sb[:], in_=bias.rearrange("(u p) -> p u", p=P))
         cast_wf(0)
-        quantize_wf(0, 0, 4)
+        quantize_wf(0, 0, 2)
+        quantize_wf(0, 2, 4)
         gather_words(1, 0)
         stage1("fine", 0, 0)
         stage1("fine", 0, 1)

@@ -19,8 +19,9 @@ ALU = mybir.AluOpType
 P = 128
 PASSES = 2
 CHUNK = 512
-PIECES = [(0, 256), (256, 256), (512, 256), (768, 256)]
+PIECES = [(0, 256), (256, 256), (512, 512)]
 N_TILES = N // P
+VECTOR_FIRST = 2
 CAST_SPLIT = (32, 88)
 
 
@@ -40,9 +41,6 @@ def tile_list_transducer_joint_logits_kernel(
         TAB0 = WF1 + 8192
         V_W10 = TAB0 + 8192
         WC_S_RAW = V_W10 + 4096
-        HB1 = WC_S_RAW + 2048
-        HB0 = HB1 + 1024
-        TH3 = HB0 + 1024
         offsets = held.tile([P, S // 16], U16, name="offsets")
         tab_s = ring.tile([P, T // 4], I32, name="tab_s", align_bytes=64, offset=TAB_S)
         wc_s_raw = ring.tile([P, PASSES * H // 4], I32, name="wc_s_raw", align_bytes=64, offset=WC_S_RAW)
@@ -186,7 +184,6 @@ def tile_list_transducer_joint_logits_kernel(
         quantize_wf(0, 2, 4)
         gather_words(1, 0)
         stage1("fine", 0, 0)
-        stage1("fine", 0, 1)
         stage1("coarse", 1, 0)
         cast_wf(1)
         quantize_wf(1, 0, 1)
@@ -199,32 +196,33 @@ def tile_list_transducer_joint_logits_kernel(
         h_w = held.tile([P, S], U32, name="h_w", align_bytes=64)
         h_s = held.tile([P, S], U8, name="h_s", align_bytes=64)
 
+        hb = {}
+
         def join_tanh(i):
             j0, n = PIECES[i]
             c, o = divmod(j0, CHUNK)
-            if i % 2:
-                th[i] = ring.tile([P, 4, n], F32, name="th%d" % i, align_bytes=64, offset=(V_W10, TH3)[i // 2])
+            if i == 1:
+                th[i] = ring.tile([P, 4, n], F32, name="th1", align_bytes=64, offset=V_W10)
             else:
-                th[i] = work.tile([P, 4, n], F32, name="th", tag="th%d" % i, bufs=1, align_bytes=64)
+                th[i] = held.tile([P, 4, n], F32, name="th%d" % i, align_bytes=64)
             for t in range(4):
                 nc.scalar.activation(th[i][:, t, :], acc[c, t][:, o : o + n], ACT.Tanh, bias=enc_sb[:, t : t + 1])
 
         def join_gain(i):
-            n = PIECES[i][1]
-            if i < 2:
-                hb = ring.tile([P, n, 4], BF16, name="hb%d" % i, align_bytes=64, offset=(HB0, HB1)[i])
-            else:
-                hb = held.tile([P, n, 4], BF16, name="hb%d" % i, align_bytes=64)
+            j0, n = PIECES[i]
+            c, o = divmod(j0, CHUNK)
+            if o == 0:
+                hb[c] = work.tile([P, CHUNK * 4], BF16, name="hb", tag="hb", bufs=1, align_bytes=64)
             nc.vector.tensor_tensor(
-                out=hb[:].rearrange("p (c i) t -> p c t i", i=4),
+                out=hb[c][:, 4 * o : 4 * (o + n)].rearrange("p (c i t) -> p c t i", i=4, t=4),
                 in0=th[i][:].rearrange("p t (c i) -> p c t i", i=4),
                 in1=gain_sb[:].unsqueeze(1).unsqueeze(3).to_broadcast([P, n // 4, 4, 4]),
                 op=ALU.mult,
             )
-            cols = slice(PIECES[i][0], PIECES[i][0] + n)
-            nc.vector.quantize_mx(
-                out=h_w[:, cols].bitcast(FP8X4), scales=h_s[:, cols], in_=hb[:].rearrange("p n t -> p (n t)")
-            )
+
+        def quantize_h(c):
+            cols = slice(c * CHUNK, (c + 1) * CHUNK)
+            nc.vector.quantize_mx(out=h_w[:, cols].bitcast(FP8X4), scales=h_s[:, cols], in_=hb[c][:])
 
         res_of = {}
 
@@ -271,30 +269,22 @@ def tile_list_transducer_joint_logits_kernel(
         join_tanh(0)
         join_gain(0)
         join_tanh(1)
-        one_bank_store(0, 2, 0, "S", 0)
         join_gain(1)
+        quantize_h(0)
+        for u in range(VECTOR_FIRST):
+            one_bank_store(u, 1, 0, "V", u)
         stage1("coarse", 1, 1)
+        stage1("fine", 0, 1)
         stage1("fine", 1, 1, stop=True)
         join_tanh(2)
         join_gain(2)
-        join_tanh(3)
-        join_gain(3)
-        one_bank_store(2, 2, 0, "S", 1)
-        for u in range(4, 8):
-            one_bank_store(u, 1, 0, "S", (u + 2) % 4)
-        for u in (8, 9):
-            open_store(u, 1, 0, 1024)
-            logits((u, 0), u, 1, 0, "S", u - 6)
-            logits((u, 0), u, 1, 512, "V", u - 4)
-            close_store(u, 0)
-        for u in (0, 2):
-            open_store(u, 2, 256, 768)
-            logits((u, 256), u, 1, 256, "S", u)
-            logits((u, 256), u + 1, 1, 256, "S", u + 1)
-            logits((u, 256), u, 2, 768, "V", 6 + u // 2)
-            close_store(u, 256)
-        for u in (4, 6):
+        quantize_h(1)
+        for u in range(VECTOR_FIRST, N_TILES):
+            one_bank_store(u, 1, 0, "S", u % 8)
+        one_bank_store(0, 1, 512, "V", 2)
+        one_bank_store(1, 1, 512, "V", 3)
+        for u in range(2, N_TILES, 2):
             open_store(u, 2, 512, 512)
-            logits((u, 512), u, 1, 512, "V", u)
-            logits((u, 512), u + 1, 1, 512, "V", u + 1)
+            logits((u, 512), u, 1, 512, "V", (u + 2) % 8)
+            logits((u, 512), u + 1, 1, 512, "S", (u + 3) % 8)
             close_store(u, 512)

@@ -36,13 +36,12 @@ def tile_list_transducer_joint_logits_kernel(
 
         ring = ctx.enter_context(tc.tile_pool(name="ring", bufs=1))
 
-        WF_BF1, GAIN, WF1 = 0, 4096, 4160
-        TAB_S = GAIN
-        TAB0 = WF1 + 8192
+        WF_BF1 = 0
+        TAB0 = 4096
         V_W10 = TAB0 + 8192
         WC_S_RAW = V_W10 + 4096
         offsets = held.tile([P, S // 16], U16, name="offsets")
-        tab_s = ring.tile([P, T // 4], I32, name="tab_s", align_bytes=64, offset=TAB_S)
+        tab_s = held.tile([P, T // 4], I32, name="tab_s", align_bytes=64)
         wc_s_raw = ring.tile([P, PASSES * H // 4], I32, name="wc_s_raw", align_bytes=64, offset=WC_S_RAW)
         warm = held.tile([P, 2], F32, name="warm")
         v_s1 = held.tile([P, S // 4], I32, name="v_s1", align_bytes=64)
@@ -61,10 +60,7 @@ def tile_list_transducer_joint_logits_kernel(
             nc.sync.dma_start(out=t_w[:], in_=tab_words[a].rearrange("p t i -> p (t i)").bitcast(I32))
 
         def load_wf(a):
-            if a == 0:
-                w = held.tile([P, 4, H], F32, name="wf_raw0", align_bytes=64)
-            else:
-                w = ring.tile([P, 4, H], F32, name="wf_raw1", align_bytes=64, offset=WF1)
+            w = held.tile([P, 4, H], F32, name="wf_raw%d" % a, align_bytes=64)
             nc.sync.dma_start(out=w[:], in_=wf[512 * a : 512 * (a + 1), :].rearrange("(p j) c -> p j c", j=4))
             return w
 
@@ -161,9 +157,9 @@ def tile_list_transducer_joint_logits_kernel(
                     stop=stop,
                 )
 
-        gather_scales()
         wf_raw.append(load_wf(1))
-        gain_sb = ring.tile([P, 4], F32, name="gain_sb", offset=GAIN)
+        gather_scales()
+        gain_sb = held.tile([P, 4], F32, name="gain_sb")
         nc.sync.dma_start(out=gain_sb[:], in_=gain.rearrange("(p t) -> p t", t=4))
         gather_words(0, 0)
         permute_wc_words()
@@ -220,9 +216,11 @@ def tile_list_transducer_joint_logits_kernel(
                 op=ALU.mult,
             )
 
-        def quantize_h(c):
-            cols = slice(c * CHUNK, (c + 1) * CHUNK)
-            nc.vector.quantize_mx(out=h_w[:, cols].bitcast(FP8X4), scales=h_s[:, cols], in_=hb[c][:])
+        def quantize_h(i):
+            j0, n = PIECES[i]
+            c, o = divmod(j0, CHUNK)
+            cols = slice(j0, j0 + n)
+            nc.vector.quantize_mx(out=h_w[:, cols].bitcast(FP8X4), scales=h_s[:, cols], in_=hb[c][:, 4 * o : 4 * (o + n)])
 
         res_of = {}
 
@@ -261,30 +259,29 @@ def tile_list_transducer_joint_logits_kernel(
             rows = slice(u0 * P, (u0 + count) * P)
             nc.sync.dma_start(out=out[rows, j0 : j0 + n].rearrange("(e p) j -> p e j", p=P), in_=res[:])
 
-        def one_bank_store(u0, count, j0, engine, bank_no):
-            open_store(u0, count, j0, CHUNK // count)
-            logits((u0, j0), u0, count, j0, engine, bank_no)
-            close_store(u0, j0)
-
         join_tanh(0)
         join_gain(0)
         join_tanh(1)
         join_gain(1)
         quantize_h(0)
-        for u in range(VECTOR_FIRST):
-            one_bank_store(u, 1, 0, "V", u)
+        quantize_h(1)
+        open_store(0, 2, 0, CHUNK)
+        logits((0, 0), 0, 1, 0, "V", 0)
+        logits((0, 0), 1, 1, 0, "V", 1)
+        close_store(0, 0)
         stage1("coarse", 1, 1)
         stage1("fine", 0, 1)
         stage1("fine", 1, 1, stop=True)
         join_tanh(2)
         join_gain(2)
-        quantize_h(1)
-        for u in range(VECTOR_FIRST, N_TILES):
-            one_bank_store(u, 1, 0, "S", u % 8)
-        one_bank_store(0, 1, 512, "V", 2)
-        one_bank_store(1, 1, 512, "V", 3)
-        for u in range(2, N_TILES, 2):
-            open_store(u, 2, 512, 512)
-            logits((u, 512), u, 1, 512, "V", (u + 2) % 8)
-            logits((u, 512), u + 1, 1, 512, "S", (u + 3) % 8)
-            close_store(u, 512)
+        quantize_h(2)
+        for u in range(VECTOR_FIRST, N_TILES, 2):
+            open_store(u, 2, 0, CHUNK)
+            logits((u, 0), u, 1, 0, "S", u % 8)
+            logits((u, 0), u + 1, 1, 0, "S", (u + 1) % 8)
+            close_store(u, 0)
+        for u0, count in ((0, 2), (2, 4), (6, 4)):
+            open_store(u0, count, CHUNK, CHUNK)
+            for u in range(u0, u0 + count):
+                logits((u0, CHUNK), u, 1, CHUNK, "V" if u < 2 or u % 2 else "S", (u + 2) % 8)
+            close_store(u0, CHUNK)

@@ -18,11 +18,12 @@ ALU = mybir.AluOpType
 
 P = 128
 PASSES = 2
-CHUNK = 512
-PIECES = [(0, 256), (256, 256), (512, 512)]
+HALF = 512
+QUARTER = 256
 N_TILES = N // P
-VECTOR_FIRST = 2
-CAST_SPLIT = (32, 88)
+CAST_SPLIT = (32, 72)
+WF_AT = (10240, 18432)
+HB_AT = (3072, 2048, 6144, 8192)
 
 
 def tile_list_transducer_joint_logits_kernel(
@@ -31,36 +32,32 @@ def tile_list_transducer_joint_logits_kernel(
     nc = tc.nc
     with ExitStack() as ctx:
         held = ctx.enter_context(tc.tile_pool(name="held", bufs=1))
-        work = ctx.enter_context(tc.tile_pool(name="work", bufs=3))
         psum = ctx.enter_context(tc.psum_pool(name="psum", bufs=1))
+        shared = ctx.enter_context(tc.tile_pool(name="shared", bufs=1))
 
-        ring = ctx.enter_context(tc.tile_pool(name="ring", bufs=1))
-
-        WF_BF1 = 0
-        TAB0 = 4096
-        V_W10 = TAB0 + 8192
-        WC_S_RAW = V_W10 + 4096
         offsets = held.tile([P, S // 16], U16, name="offsets")
         tab_s = held.tile([P, T // 4], I32, name="tab_s", align_bytes=64)
-        wc_s_raw = ring.tile([P, PASSES * H // 4], I32, name="wc_s_raw", align_bytes=64, offset=WC_S_RAW)
-        warm = held.tile([P, 2], F32, name="warm")
+        wc_s_raw = shared.tile([P, PASSES * H // 4], I32, name="wc_s_raw", align_bytes=64, offset=0)
         v_s1 = held.tile([P, S // 4], I32, name="v_s1", align_bytes=64)
+        warm = held.tile([P, 2], F32, name="warm")
         nc.gpsimd.memset(tab_s[:], 0)
         nc.vector.memset(warm[:, 0:1], 0.0)
         nc.vector.memset(wc_s_raw[:], 0)
         nc.vector.memset(v_s1[:], 0)
         nc.scalar.activation(warm[:, 1:2], warm[:, 0:1], ACT.Tanh)
 
-        def load_scale_rows(dst, src):
+        def load_scale_rows(queue, dst, src):
             rows = src.bitcast(I32).rearrange("a (q r) c -> r q a c", r=4)
             for r in range(4):
-                nc.sync.dma_start(out=dst[r:P:32, :].rearrange("q (a c) -> q a c", a=src.shape[0]), in_=rows[r])
+                queue.dma_start(out=dst[r:P:32, :].rearrange("q (a c) -> q a c", a=src.shape[0]), in_=rows[r])
 
-        def load_table_words(t_w, a):
-            nc.sync.dma_start(out=t_w[:], in_=tab_words[a].rearrange("p t i -> p (t i)").bitcast(I32))
+        def load_table_words(a):
+            words = held.tile([P, T], I32, name="tab_w%d" % a, align_bytes=64)
+            nc.sync.dma_start(out=words[:], in_=tab_words[a].rearrange("p t i -> p (t i)").bitcast(I32))
+            return words
 
         def load_wf(a):
-            w = held.tile([P, 4, H], F32, name="wf_raw%d" % a, align_bytes=64)
+            w = shared.tile([P, 4, H], F32, name="wf_raw%d" % a, align_bytes=64, offset=WF_AT[a])
             nc.sync.dma_start(out=w[:], in_=wf[512 * a : 512 * (a + 1), :].rearrange("(p j) c -> p j c", j=4))
             return w
 
@@ -70,166 +67,134 @@ def tile_list_transducer_joint_logits_kernel(
         tab_rows = tab_scales.bitcast(I32).rearrange("a (q r) c -> r q a c", r=4)
         for r in range(4):
             nc.sync.dma_start(out=tab_s[r:P:16, :], in_=tab_rows[r])
-        tab_w0 = ring.tile([P, T], I32, name="tab_w0", align_bytes=64, offset=TAB0)
-        tab_w1 = held.tile([P, T], I32, name="tab_w1", align_bytes=64)
-        tab_w = [tab_w0, tab_w1]
-        load_table_words(tab_w[0], 0)
+        tab_w = [load_table_words(0)]
         wc_raw = held.tile([P, PASSES, H // 2], I32, name="wc_raw", align_bytes=64)
         nc.sync.dma_start(out=wc_raw[:], in_=wc_words.bitcast(I32).rearrange("a p c -> p a c"))
-        load_scale_rows(wc_s_raw, wc_scales)
-        wf_raw = [load_wf(0)]
-        load_table_words(tab_w[1], 1)
-
-        v_w = {}
-        v_s01 = held.tile([P, S], U8, name="v_s01", align_bytes=64)
-        v_s = {}
-        for c in range(2):
-            v_s[0, c] = v_s01[:, c * CHUNK : (c + 1) * CHUNK]
-            v_s[1, c] = v_s1[:].bitcast(U8)[:, c * CHUNK : (c + 1) * CHUNK]
-
-        def gather_scales():
-            nc.vector.tensor_copy(v_s01[:], tab_s[:].bitcast(U8).indirect(offsets[:]))
-            for r in range(4):
-                nc.sync.dma_start(out=v_s1[r:P:32, :], in_=v_s01[:].bitcast(I32)[16 + r : P : 32, :])
-
-        def gather_words(a, c):
-            if c == 1:
-                g = ring.tile([P, CHUNK], U32, name="v_w%d1" % a, align_bytes=64, offset=(WC_S_RAW, WF_BF1)[a])
-            elif (a, c) == (1, 0):
-                g = ring.tile([P, CHUNK], U32, name="v_w10", align_bytes=64, offset=V_W10)
-            else:
-                g = held.tile([P, CHUNK], U32, name="v_w%d%d" % (a, c), align_bytes=64)
-            nc.vector.tensor_copy(g[:], tab_w[a][:].bitcast(U32).indirect(offsets[:, 32 * c : 32 * (c + 1)]))
-            v_w[a, c] = g
+        load_scale_rows(nc.sync, wc_s_raw, wc_scales)
+        wf_raw = [load_wf(0), load_wf(1)]
 
         wc_w = held.tile([P, PASSES, 4, 2 * P], U8, name="wc_w", align_bytes=64)
-        wc_s = held.tile([P, PASSES, 4, P], U8, name="wc_s", align_bytes=64)
+        v_s0 = held.tile([P, S], U8, name="v_s0", align_bytes=64)
+        nc.vector.tensor_copy(v_s0[:], tab_s[:].bitcast(U8).indirect(offsets[:]))
+        for r in range(4):
+            nc.sync.dma_start(out=v_s1[r:P:32, :], in_=v_s0[:].bitcast(I32)[16 + r : P : 32, :])
+        v_s = {}
+        for q in range(4):
+            v_s[0, q] = v_s0[:, q * QUARTER : (q + 1) * QUARTER]
+            v_s[1, q] = v_s1[:].bitcast(U8)[:, q * QUARTER : (q + 1) * QUARTER]
+        tab_w.append(load_table_words(1))
+        gain_sb = held.tile([P, 4], F32, name="gain_sb")
+        nc.sync.dma_start(out=gain_sb[:], in_=gain.rearrange("(p t) -> p t", t=4))
+        wj_w = held.tile([P, N], I32, name="wj_w", align_bytes=64)
+        nc.sync.dma_start(out=wj_w[:], in_=wj_words[0].rearrange("p c i -> p (c i)").bitcast(I32))
+        bias_sb = held.tile([P, N_TILES], F32, name="bias_sb")
+        with nc.allow_non_contiguous_dma(reason="one bias value for each partition and output tile"):
+            nc.sync.dma_start(out=bias_sb[:], in_=bias.rearrange("(u p) -> p u", p=P))
 
-        def permute_wc_words():
-            nc.vector.tensor_copy(
-                out=wc_w[:].bitcast(U16),
-                in_=wc_raw[:].bitcast(U16).rearrange("p a (m t) -> p a t m", t=4),
-            )
+        v_w = {}
 
-        def permute_wc_scales():
-            nc.vector.tensor_copy(
-                out=wc_s[:],
-                in_=wc_s_raw[:].bitcast(U8).rearrange("p (a m t) -> p a t m", a=PASSES, t=4),
-            )
+        def gather_words(a, dst, j0, n):
+            nc.vector.tensor_copy(dst[:], tab_w[a][:].bitcast(U32).indirect(offsets[:, j0 // 16 : (j0 + n) // 16]))
+            for lo in range(0, n, QUARTER):
+                v_w[a, (j0 + lo) // QUARTER] = dst[:, lo : lo + QUARTER]
 
-        wf_bf0 = held.tile([P, 4, P, 4], BF16, name="wf_bf0", align_bytes=64)
-        wf_bf1 = ring.tile([P, 4, P, 4], BF16, name="wf_bf1", align_bytes=64, offset=WF_BF1)
-        wf_bf = [wf_bf0, wf_bf1]
         wf_w = [held.tile([P, 4, P], U32, name="wf_w%d" % a, align_bytes=64) for a in range(PASSES)]
         wf_s = [held.tile([P, 4, P], U8, name="wf_s%d" % a, align_bytes=64) for a in range(PASSES)]
 
-        def cast_wf(a):
+        def quantize_wf(a):
+            rounded = held.tile([P, 4, P, 4], BF16, name="wf_bf%d" % a, align_bytes=64)
             for copy, m0, m1 in ((nc.vector.tensor_copy, 0, CAST_SPLIT[a]), (nc.scalar.copy, CAST_SPLIT[a], P)):
                 copy(
-                    out=wf_bf[a][:, :, m0:m1, :].rearrange("p t m j -> p m j t"),
+                    out=rounded[:, :, m0:m1, :].rearrange("p t m j -> p m j t"),
                     in_=wf_raw[a][:].rearrange("p j (m t) -> p m j t", t=4)[:, m0:m1, :, :],
                 )
+            for t0 in (0, 2):
+                nc.vector.quantize_mx(
+                    out=wf_w[a][:, t0 : t0 + 2, :].rearrange("p t m -> p (t m)").bitcast(FP8X4),
+                    scales=wf_s[a][:, t0 : t0 + 2, :].rearrange("p t m -> p (t m)"),
+                    in_=rounded[:, t0 : t0 + 2, :, :].rearrange("p t m j -> p (t m j)"),
+                )
 
-        def quantize_wf(a, t0, t1):
-            nc.vector.quantize_mx(
-                out=wf_w[a][:, t0:t1, :].rearrange("p t m -> p (t m)").bitcast(FP8X4),
-                scales=wf_s[a][:, t0:t1, :].rearrange("p t m -> p (t m)"),
-                in_=wf_bf[a][:, t0:t1, :, :].rearrange("p t m j -> p (t m j)"),
-            )
+        sums = {}
 
-        acc = {}
-
-        def stage1(kind, a, c, start=False, stop=False):
-            for t in range(4):
-                if start:
-                    acc[c, t] = psum.tile([P, CHUNK], F32, name="acc", tag="bank%d" % (4 * c + t))
+        def project(kind, a, q, pair, start=False, stop=False):
+            if start:
+                sums[q, pair] = psum.tile([P, 2, QUARTER], F32, name="sums", tag="bank%d" % (2 * q + pair))
+            scales = v_s[a, q]
+            n = P if kind == "coarse" else QUARTER
+            steps = [(e, lo) for e in range(2) for lo in range(0, QUARTER, n)]
+            for e, lo in steps:
+                t = 2 * pair + e
                 if kind == "coarse":
                     lhsT, lhsT_scale = wc_w[:, a, t, :].bitcast(FP4X4), wc_s[:, a, t, :]
                 else:
                     lhsT, lhsT_scale = wf_w[a][:, t, :].bitcast(FP8X4), wf_s[a][:, t, :]
                 nc.tensor.matmul_mx(
-                    out=acc[c, t][:],
+                    out=sums[q, pair][:, e, lo : lo + n],
                     lhsT=lhsT,
                     lhsT_scale=lhsT_scale,
-                    rhs=v_w[a, c][:].bitcast(FP8X4),
-                    rhs_scale=v_s[a, c],
-                    start=start,
-                    stop=stop,
+                    rhs=v_w[a, q][:, lo : lo + n].bitcast(FP8X4),
+                    rhs_scale=scales[:, lo : lo + n],
+                    start=start and (e, lo) == steps[0],
+                    stop=stop and (e, lo) == steps[-1],
                 )
 
-        wf_raw.append(load_wf(1))
-        gather_scales()
-        gain_sb = held.tile([P, 4], F32, name="gain_sb")
-        nc.sync.dma_start(out=gain_sb[:], in_=gain.rearrange("(p t) -> p t", t=4))
-        gather_words(0, 0)
-        permute_wc_words()
-        permute_wc_scales()
-        stage1("coarse", 0, 0, start=True)
-        gather_words(0, 1)
-        stage1("coarse", 0, 1, start=True)
-        wj_w = ring.tile([P, N], I32, name="wj_w", align_bytes=64, offset=TAB0)
-        wj_s = ring.tile([P, N // 4], I32, name="wj_s", align_bytes=64, offset=TAB0 + 4 * N)
-        nc.sync.dma_start(out=wj_w[:], in_=wj_words[0].rearrange("p c i -> p (c i)").bitcast(I32))
+        gather_words(0, held.tile([P, HALF], U32, name="v_w00", align_bytes=64), 0, HALF)
+        nc.vector.tensor_copy(
+            out=wc_w[:].bitcast(U16),
+            in_=wc_raw[:].bitcast(U16).rearrange("p a (m t) -> p a t m", t=4),
+        )
+        wc_s = held.tile([P, PASSES, 4, P], U8, name="wc_s", align_bytes=64)
+        nc.vector.tensor_copy(
+            out=wc_s[:],
+            in_=wc_s_raw[:].bitcast(U8).rearrange("p (a m t) -> p a t m", a=PASSES, t=4),
+        )
+        gather_words(0, shared.tile([P, HALF], U32, name="v_w01", align_bytes=64, offset=0), HALF, HALF)
+        banks = [(q, pair) for q in range(4) for pair in range(2)]
+        for q, pair in banks:
+            project("coarse", 0, q, pair, start=True)
+        quantize_wf(0)
+        for q, pair in banks:
+            project("fine", 0, q, pair)
+        quantize_wf(1)
+        wj_s = shared.tile([P, N // 4], I32, name="wj_s", align_bytes=64, offset=WF_AT[1])
         nc.vector.memset(wj_s[:], 0)
-        load_scale_rows(wj_s, wj_scales)
-        bias_sb = held.tile([P, N_TILES], F32, name="bias_sb")
-        with nc.allow_non_contiguous_dma(reason="one bias value for each partition and output tile"):
-            nc.sync.dma_start(out=bias_sb[:], in_=bias.rearrange("(u p) -> p u", p=P))
-        cast_wf(0)
-        quantize_wf(0, 0, 2)
-        quantize_wf(0, 2, 4)
-        gather_words(1, 0)
-        stage1("fine", 0, 0)
-        stage1("coarse", 1, 0)
-        cast_wf(1)
-        quantize_wf(1, 0, 1)
-        quantize_wf(1, 1, 2)
-        quantize_wf(1, 2, 4)
-        stage1("fine", 1, 0, stop=True)
-        gather_words(1, 1)
+        load_scale_rows(nc.scalar, wj_s, wj_scales)
+        for q in range(4):
+            gather_words(1, held.tile([P, QUARTER], U32, name="v_w1%d" % q, align_bytes=64), q * QUARTER, QUARTER)
 
-        th = {}
+        def finish_sums(q):
+            for pair in range(2):
+                project("coarse", 1, q, pair)
+                project("fine", 1, q, pair, stop=True)
+
         h_w = held.tile([P, S], U32, name="h_w", align_bytes=64)
         h_s = held.tile([P, S], U8, name="h_s", align_bytes=64)
-
+        th = {}
         hb = {}
 
-        def join_tanh(i):
-            j0, n = PIECES[i]
-            c, o = divmod(j0, CHUNK)
-            if i == 1:
-                th[i] = ring.tile([P, 4, n], F32, name="th1", align_bytes=64, offset=V_W10)
-            else:
-                th[i] = held.tile([P, 4, n], F32, name="th%d" % i, align_bytes=64)
+        def join_tanh(q):
+            th[q] = held.tile([P, 4, QUARTER], F32, name="th", tag="th%d" % (0, 1, 2, 1)[q], align_bytes=64)
             for t in range(4):
-                nc.scalar.activation(th[i][:, t, :], acc[c, t][:, o : o + n], ACT.Tanh, bias=enc_sb[:, t : t + 1])
+                nc.scalar.activation(th[q][:, t, :], sums[q, t // 2][:, t % 2, :], ACT.Tanh, bias=enc_sb[:, t : t + 1])
 
-        def join_gain(i):
-            j0, n = PIECES[i]
-            c, o = divmod(j0, CHUNK)
-            if o == 0:
-                hb[c] = work.tile([P, CHUNK * 4], BF16, name="hb", tag="hb", bufs=1, align_bytes=64)
-            nc.vector.tensor_tensor(
-                out=hb[c][:, 4 * o : 4 * (o + n)].rearrange("p (c i t) -> p c t i", i=4, t=4),
-                in0=th[i][:].rearrange("p t (c i) -> p c t i", i=4),
-                in1=gain_sb[:].unsqueeze(1).unsqueeze(3).to_broadcast([P, n // 4, 4, 4]),
-                op=ALU.mult,
-            )
+        def join_gain(q, cuts):
+            for lo, hi in cuts:
+                hb[q, lo] = shared.tile([P, 4 * (hi - lo)], BF16, name="hb%d_%d" % (q, lo), align_bytes=64, offset=HB_AT[q] + 8 * lo)
+                nc.vector.tensor_tensor(
+                    out=hb[q, lo][:].rearrange("p (c i t) -> p c t i", i=4, t=4),
+                    in0=th[q][:, :, lo:hi].rearrange("p t (c i) -> p c t i", i=4),
+                    in1=gain_sb[:].unsqueeze(1).unsqueeze(3).to_broadcast([P, (hi - lo) // 4, 4, 4]),
+                    op=ALU.mult,
+                )
 
-        def quantize_h(i):
-            j0, n = PIECES[i]
-            c, o = divmod(j0, CHUNK)
-            cols = slice(j0, j0 + n)
-            nc.vector.quantize_mx(out=h_w[:, cols].bitcast(FP8X4), scales=h_s[:, cols], in_=hb[c][:, 4 * o : 4 * (o + n)])
+        def quantize_h(q, cuts):
+            for lo, hi in cuts:
+                cols = slice(q * QUARTER + lo, q * QUARTER + hi)
+                nc.vector.quantize_mx(out=h_w[:, cols].bitcast(FP8X4), scales=h_s[:, cols], in_=hb[q, lo][:])
 
-        res_of = {}
-
-        def open_store(u0, count, j0, n):
-            res_of[u0, j0] = held.tile([P, count, n], F32, name="res%d_%d" % (u0, j0))
-
-        def logits(store, u0, count, j0, engine, bank_no):
-            n = CHUNK // count
-            res = res_of[store][:, u0 - store[0] : u0 - store[0] + count, j0 - store[1] : j0 - store[1] + n]
+        def logits(res, u0, j0, engine, bank_no):
+            count, n = res.shape[1], res.shape[2]
             bank = psum.tile([P, count, n], F32, name="bank", tag="bank%d" % bank_no)
             for e in range(count):
                 u = u0 + e
@@ -253,35 +218,41 @@ def tile_list_transducer_joint_logits_kernel(
                 for e in range(count):
                     nc.scalar.activation(res[:, e, :], bank[:, e, :], ACT.Identity, bias=bias_sb[:, u0 + e : u0 + e + 1])
 
-        def close_store(u0, j0):
-            res = res_of[u0, j0]
-            count, n = res.shape[1], res.shape[2]
+        def store(u0, j0, n, plan):
+            per_bank = HALF // n
+            count = per_bank * len(plan)
+            res = held.tile([P, count, n], F32, name="res%d_%d" % (u0, j0))
+            for b, (engine, bank_no) in enumerate(plan):
+                logits(res[:, per_bank * b : per_bank * (b + 1), :], u0 + per_bank * b, j0, engine, bank_no)
             rows = slice(u0 * P, (u0 + count) * P)
             nc.sync.dma_start(out=out[rows, j0 : j0 + n].rearrange("(e p) j -> p e j", p=P), in_=res[:])
 
+        whole = [(0, QUARTER)]
+        halves = [(0, P), (P, QUARTER)]
+        finish_sums(0)
         join_tanh(0)
-        join_gain(0)
+        finish_sums(1)
+        join_gain(0, halves)
+        quantize_h(0, halves)
+        last_scales = shared.tile([P, QUARTER // 4], I32, name="last_scales", align_bytes=64, offset=HB_AT[0] + 8 * P)
+        nc.vector.tensor_copy(last_scales[:], v_s[1, 3].bitcast(I32))
+        v_s[1, 3] = last_scales[:].bitcast(U8)
         join_tanh(1)
-        join_gain(1)
-        quantize_h(0)
-        quantize_h(1)
-        open_store(0, 2, 0, CHUNK)
-        logits((0, 0), 0, 1, 0, "V", 0)
-        logits((0, 0), 1, 1, 0, "V", 1)
-        close_store(0, 0)
-        stage1("coarse", 1, 1)
-        stage1("fine", 0, 1)
-        stage1("fine", 1, 1, stop=True)
+        join_gain(1, whole)
+        store(0, 0, QUARTER, [("S", 0), ("V", 1)])
+        quantize_h(1, whole)
+        finish_sums(2)
         join_tanh(2)
-        join_gain(2)
-        quantize_h(2)
-        for u in range(VECTOR_FIRST, N_TILES, 2):
-            open_store(u, 2, 0, CHUNK)
-            logits((u, 0), u, 1, 0, "S", u % 8)
-            logits((u, 0), u + 1, 1, 0, "S", (u + 1) % 8)
-            close_store(u, 0)
-        for u0, count in ((0, 2), (2, 4), (6, 4)):
-            open_store(u0, count, CHUNK, CHUNK)
-            for u in range(u0, u0 + count):
-                logits((u0, CHUNK), u, 1, CHUNK, "V" if u < 2 or u % 2 else "S", (u + 2) % 8)
-            close_store(u0, CHUNK)
+        store(4, 0, QUARTER, [("S", 2), ("V", 3)])
+        finish_sums(3)
+        join_tanh(3)
+        store(0, QUARTER, QUARTER, [("V", 0), ("S", 1)])
+        join_gain(2, whole)
+        join_gain(3, whole)
+        quantize_h(2, whole)
+        quantize_h(3, whole)
+        store(4, QUARTER, QUARTER, [("S", 2), ("S", 3)])
+        store(8, 0, HALF, [("S", 4), ("S", 5)])
+        store(0, HALF, HALF, [("V", 6), ("S", 7)])
+        store(2, HALF, HALF, [("V", 0), ("S", 1), ("V", 2), ("S", 3)])
+        store(6, HALF, HALF, [("V", 4), ("S", 5), ("V", 6), ("S", 7)])

@@ -21,7 +21,7 @@ PASSES = 2
 HALF = 512
 QUARTER = 256
 N_TILES = N // P
-CAST_SPLIT = (32, 72)
+CAST_SPLIT = (44, 64)
 WF_AT = (10240, 18432)
 HB_AT = (3072, 2048, 6144, 8192)
 
@@ -72,6 +72,7 @@ def tile_list_transducer_joint_logits_kernel(
         nc.sync.dma_start(out=wc_raw[:], in_=wc_words.bitcast(I32).rearrange("a p c -> p a c"))
         load_scale_rows(nc.sync, wc_s_raw, wc_scales)
         wf_raw = [load_wf(0), load_wf(1)]
+        tab_w.append(load_table_words(1))
 
         wc_w = held.tile([P, PASSES, 4, 2 * P], U8, name="wc_w", align_bytes=64)
         v_s0 = held.tile([P, S], U8, name="v_s0", align_bytes=64)
@@ -82,7 +83,6 @@ def tile_list_transducer_joint_logits_kernel(
         for q in range(4):
             v_s[0, q] = v_s0[:, q * QUARTER : (q + 1) * QUARTER]
             v_s[1, q] = v_s1[:].bitcast(U8)[:, q * QUARTER : (q + 1) * QUARTER]
-        tab_w.append(load_table_words(1))
         gain_sb = held.tile([P, 4], F32, name="gain_sb")
         nc.sync.dma_start(out=gain_sb[:], in_=gain.rearrange("(p t) -> p t", t=4))
         wj_w = held.tile([P, N], I32, name="wj_w", align_bytes=64)
@@ -218,14 +218,17 @@ def tile_list_transducer_joint_logits_kernel(
                 for e in range(count):
                     nc.scalar.activation(res[:, e, :], bank[:, e, :], ACT.Identity, bias=bias_sb[:, u0 + e : u0 + e + 1])
 
-        def store(u0, j0, n, plan):
-            per_bank = HALF // n
-            count = per_bank * len(plan)
-            res = held.tile([P, count, n], F32, name="res%d_%d" % (u0, j0))
-            for b, (engine, bank_no) in enumerate(plan):
-                logits(res[:, per_bank * b : per_bank * (b + 1), :], u0 + per_bank * b, j0, engine, bank_no)
+        def write_out(res, u0, j0):
+            count, n = res.shape[1], res.shape[2]
             rows = slice(u0 * P, (u0 + count) * P)
             nc.sync.dma_start(out=out[rows, j0 : j0 + n].rearrange("(e p) j -> p e j", p=P), in_=res[:])
+
+        def store(u0, j0, n, plan):
+            per_bank = HALF // n
+            res = held.tile([P, per_bank * len(plan), n], F32, name="res%d_%d" % (u0, j0))
+            for b, (engine, bank_no) in enumerate(plan):
+                logits(res[:, per_bank * b : per_bank * (b + 1), :], u0 + per_bank * b, j0, engine, bank_no)
+            write_out(res, u0, j0)
 
         whole = [(0, QUARTER)]
         halves = [(0, P), (P, QUARTER)]
@@ -239,20 +242,24 @@ def tile_list_transducer_joint_logits_kernel(
         v_s[1, 3] = last_scales[:].bitcast(U8)
         join_tanh(1)
         join_gain(1, whole)
-        store(0, 0, QUARTER, [("S", 0), ("V", 1)])
+        store(2, 0, QUARTER, [("S", 0), ("V", 1)])
         quantize_h(1, whole)
         finish_sums(2)
         join_tanh(2)
-        store(4, 0, QUARTER, [("S", 2), ("V", 3)])
+        store(6, 0, QUARTER, [("S", 2), ("V", 3)])
         finish_sums(3)
         join_tanh(3)
-        store(0, QUARTER, QUARTER, [("V", 0), ("S", 1)])
         join_gain(2, whole)
         join_gain(3, whole)
         quantize_h(2, whole)
         quantize_h(3, whole)
-        store(4, QUARTER, QUARTER, [("S", 2), ("S", 3)])
-        store(8, 0, HALF, [("S", 4), ("S", 5)])
+        store(2, QUARTER, QUARTER, [("S", 0), ("S", 1)])
+        store(0, 0, HALF, [("S", 4), ("S", 5)])
         store(0, HALF, HALF, [("V", 6), ("S", 7)])
-        store(2, HALF, HALF, [("V", 0), ("S", 1), ("V", 2), ("S", 3)])
-        store(6, HALF, HALF, [("V", 4), ("S", 5), ("V", 6), ("S", 7)])
+        store(2, HALF, HALF, [("V", 0), ("S", 1), ("V", 4), ("S", 5)])
+        rest = held.tile([P, 4, S - QUARTER], F32, name="rest")
+        logits(rest[:, 0:2, 0:QUARTER], 6, QUARTER, "V", 2)
+        for e in range(4):
+            logits(rest[:, e : e + 1, QUARTER:], 6 + e, HALF, "VS"[e % 2], (6, 7, 0, 1)[e])
+        logits(rest[:, 2:4, 0:QUARTER], 8, QUARTER, "V", 4)
+        write_out(rest, 6, QUARTER)

@@ -23,7 +23,7 @@ QUARTER = 256
 N_TILES = N // P
 CAST_SPLIT = (44, 64)
 WF_AT = (10240, 18432)
-HB_AT = (3072, 2048, 6144, 8192)
+HB_AT = (3072, 1792, 6144, 8192)
 
 
 def tile_list_transducer_joint_logits_kernel(
@@ -237,24 +237,28 @@ def tile_list_transducer_joint_logits_kernel(
         finish_sums(1)
         join_gain(0, halves)
         quantize_h(0, halves)
-        last_scales = shared.tile([P, QUARTER // 4], I32, name="last_scales", align_bytes=64, offset=HB_AT[0] + 8 * P)
+        last_scales = shared.tile([P, QUARTER // 4], I32, name="last_scales", align_bytes=64, offset=HB_AT[0] + 8 * P - QUARTER)
         nc.vector.tensor_copy(last_scales[:], v_s[1, 3].bitcast(I32))
         v_s[1, 3] = last_scales[:].bitcast(U8)
         join_tanh(1)
         join_gain(1, whole)
-        store(2, 0, QUARTER, [("S", 0), ("V", 1)])
+        store(6, 0, QUARTER, [("S", 0), ("V", 1)])
         quantize_h(1, whole)
         finish_sums(2)
         join_tanh(2)
-        store(6, 0, QUARTER, [("S", 2), ("V", 3)])
+        store(0, 0, HALF, [("S", 2)])
+        third = held.tile([P, 2, HALF], F32, name="third")
+        logits(third[:, 0:1, :], 1, 0, "V", 3)
         finish_sums(3)
         join_tanh(3)
         join_gain(2, whole)
         join_gain(3, whole)
         quantize_h(2, whole)
         quantize_h(3, whole)
-        store(2, QUARTER, QUARTER, [("S", 0), ("S", 1)])
-        store(0, 0, HALF, [("S", 4), ("S", 5)])
+        logits(third[:, 1:2, :], 2, 0, "S", 0)
+        write_out(third, 1, 0)
+        store(3, 0, HALF, [("S", 1), ("S", 4)])
+        store(5, 0, HALF, [("S", 5)])
         store(0, HALF, HALF, [("V", 6), ("S", 7)])
         store(2, HALF, HALF, [("V", 0), ("S", 1), ("V", 4), ("S", 5)])
         rest = held.tile([P, 4, S - QUARTER], F32, name="rest")

@@ -23,7 +23,10 @@ QUARTER = 256
 N_TILES = N // P
 CAST_SPLIT = (44, 64)
 WF_AT = (10240, 18432)
-HB_AT = (3072, 1792, 6144, 8192)
+PIECES = ((0, 128), (128, 256), (256, 384), (384, 512), (512, 768), (768, 1024))
+FIRST_BANK = (0, 1, 2, 3, 4, 6)
+HB_AT = (2048, 3072, 2048, 4096, 5120, 7168)
+RES_Y_AT = 2048 - 1024
 
 
 def tile_list_transducer_joint_logits_kernel(
@@ -79,10 +82,7 @@ def tile_list_transducer_joint_logits_kernel(
         nc.vector.tensor_copy(v_s0[:], tab_s[:].bitcast(U8).indirect(offsets[:]))
         for r in range(4):
             nc.sync.dma_start(out=v_s1[r:P:32, :], in_=v_s0[:].bitcast(I32)[16 + r : P : 32, :])
-        v_s = {}
-        for q in range(4):
-            v_s[0, q] = v_s0[:, q * QUARTER : (q + 1) * QUARTER]
-            v_s[1, q] = v_s1[:].bitcast(U8)[:, q * QUARTER : (q + 1) * QUARTER]
+        v_s = [v_s0[:], v_s1[:].bitcast(U8)]
         gain_sb = held.tile([P, 4], F32, name="gain_sb")
         nc.sync.dma_start(out=gain_sb[:], in_=gain.rearrange("(p t) -> p t", t=4))
         wj_w = held.tile([P, N], I32, name="wj_w", align_bytes=64)
@@ -95,8 +95,9 @@ def tile_list_transducer_joint_logits_kernel(
 
         def gather_words(a, dst, j0, n):
             nc.vector.tensor_copy(dst[:], tab_w[a][:].bitcast(U32).indirect(offsets[:, j0 // 16 : (j0 + n) // 16]))
-            for lo in range(0, n, QUARTER):
-                v_w[a, (j0 + lo) // QUARTER] = dst[:, lo : lo + QUARTER]
+            for k, (lo, hi) in enumerate(PIECES):
+                if j0 <= lo and hi <= j0 + n:
+                    v_w[a, k] = dst[:, lo - j0 : hi - j0]
 
         wf_w = [held.tile([P, 4, P], U32, name="wf_w%d" % a, align_bytes=64) for a in range(PASSES)]
         wf_s = [held.tile([P, 4, P], U8, name="wf_s%d" % a, align_bytes=64) for a in range(PASSES)]
@@ -117,26 +118,33 @@ def tile_list_transducer_joint_logits_kernel(
 
         sums = {}
 
-        def project(kind, a, q, pair, start=False, stop=False):
+        def bank_tiles(k):
+            lo, hi = PIECES[k]
+            per_bank = HALF // (hi - lo)
+            return [range(t0, t0 + per_bank) for t0 in range(0, 4, per_bank)]
+
+        def project(kind, a, k, b, start=False, stop=False):
+            lo, hi = PIECES[k]
+            tiles = bank_tiles(k)[b]
             if start:
-                sums[q, pair] = psum.tile([P, 2, QUARTER], F32, name="sums", tag="bank%d" % (2 * q + pair))
-            scales = v_s[a, q]
-            n = P if kind == "coarse" else QUARTER
-            steps = [(e, lo) for e in range(2) for lo in range(0, QUARTER, n)]
-            for e, lo in steps:
-                t = 2 * pair + e
+                bank = psum.tile([P, len(tiles), hi - lo], F32, name="sums", tag="bank%d" % (FIRST_BANK[k] + b))
+                for e, t in enumerate(tiles):
+                    sums[k, t] = bank[:, e, :]
+            n = P if kind == "coarse" else hi - lo
+            steps = [(t, c) for t in tiles for c in range(0, hi - lo, n)]
+            for t, c in steps:
                 if kind == "coarse":
                     lhsT, lhsT_scale = wc_w[:, a, t, :].bitcast(FP4X4), wc_s[:, a, t, :]
                 else:
                     lhsT, lhsT_scale = wf_w[a][:, t, :].bitcast(FP8X4), wf_s[a][:, t, :]
                 nc.tensor.matmul_mx(
-                    out=sums[q, pair][:, e, lo : lo + n],
+                    out=sums[k, t][:, c : c + n],
                     lhsT=lhsT,
                     lhsT_scale=lhsT_scale,
-                    rhs=v_w[a, q][:, lo : lo + n].bitcast(FP8X4),
-                    rhs_scale=scales[:, lo : lo + n],
-                    start=start and (e, lo) == steps[0],
-                    stop=stop and (e, lo) == steps[-1],
+                    rhs=v_w[a, k][:, c : c + n].bitcast(FP8X4),
+                    rhs_scale=v_s[a][:, lo + c : lo + c + n],
+                    start=start and (t, c) == steps[0],
+                    stop=stop and (t, c) == steps[-1],
                 )
 
         gather_words(0, held.tile([P, HALF], U32, name="v_w00", align_bytes=64), 0, HALF)
@@ -150,12 +158,12 @@ def tile_list_transducer_joint_logits_kernel(
             in_=wc_s_raw[:].bitcast(U8).rearrange("p (a m t) -> p a t m", a=PASSES, t=4),
         )
         gather_words(0, shared.tile([P, HALF], U32, name="v_w01", align_bytes=64, offset=0), HALF, HALF)
-        banks = [(q, pair) for q in range(4) for pair in range(2)]
-        for q, pair in banks:
-            project("coarse", 0, q, pair, start=True)
+        banks = [(k, b) for k in range(len(PIECES)) for b in range(len(bank_tiles(k)))]
+        for k, b in banks:
+            project("coarse", 0, k, b, start=True)
         quantize_wf(0)
-        for q, pair in banks:
-            project("fine", 0, q, pair)
+        for k, b in banks:
+            project("fine", 0, k, b)
         quantize_wf(1)
         wj_s = shared.tile([P, N // 4], I32, name="wj_s", align_bytes=64, offset=WF_AT[1])
         nc.vector.memset(wj_s[:], 0)
@@ -163,35 +171,35 @@ def tile_list_transducer_joint_logits_kernel(
         for q in range(4):
             gather_words(1, held.tile([P, QUARTER], U32, name="v_w1%d" % q, align_bytes=64), q * QUARTER, QUARTER)
 
-        def finish_sums(q):
-            for pair in range(2):
-                project("coarse", 1, q, pair)
-                project("fine", 1, q, pair, stop=True)
+        def finish_sums(k):
+            for b in range(len(bank_tiles(k))):
+                project("coarse", 1, k, b)
+                project("fine", 1, k, b, stop=True)
 
         h_w = held.tile([P, S], U32, name="h_w", align_bytes=64)
         h_s = held.tile([P, S], U8, name="h_s", align_bytes=64)
         th = {}
         hb = {}
 
-        def join_tanh(q):
-            th[q] = held.tile([P, 4, QUARTER], F32, name="th", tag="th%d" % (0, 1, 2, 1)[q], align_bytes=64)
+        def join_tanh(k):
+            lo, hi = PIECES[k]
+            th[k] = held.tile([P, 4, hi - lo], F32, name="th%d" % k, align_bytes=64)
             for t in range(4):
-                nc.scalar.activation(th[q][:, t, :], sums[q, t // 2][:, t % 2, :], ACT.Tanh, bias=enc_sb[:, t : t + 1])
+                nc.scalar.activation(th[k][:, t, :], sums[k, t], ACT.Tanh, bias=enc_sb[:, t : t + 1])
 
-        def join_gain(q, cuts):
-            for lo, hi in cuts:
-                hb[q, lo] = shared.tile([P, 4 * (hi - lo)], BF16, name="hb%d_%d" % (q, lo), align_bytes=64, offset=HB_AT[q] + 8 * lo)
-                nc.vector.tensor_tensor(
-                    out=hb[q, lo][:].rearrange("p (c i t) -> p c t i", i=4, t=4),
-                    in0=th[q][:, :, lo:hi].rearrange("p t (c i) -> p c t i", i=4),
-                    in1=gain_sb[:].unsqueeze(1).unsqueeze(3).to_broadcast([P, (hi - lo) // 4, 4, 4]),
-                    op=ALU.mult,
-                )
+        def join_gain(k):
+            lo, hi = PIECES[k]
+            hb[k] = shared.tile([P, 4 * (hi - lo)], BF16, name="hb%d" % k, align_bytes=64, offset=HB_AT[k])
+            nc.vector.tensor_tensor(
+                out=hb[k][:].rearrange("p (c i t) -> p c t i", i=4, t=4),
+                in0=th[k][:].rearrange("p t (c i) -> p c t i", i=4),
+                in1=gain_sb[:].unsqueeze(1).unsqueeze(3).to_broadcast([P, (hi - lo) // 4, 4, 4]),
+                op=ALU.mult,
+            )
 
-        def quantize_h(q, cuts):
-            for lo, hi in cuts:
-                cols = slice(q * QUARTER + lo, q * QUARTER + hi)
-                nc.vector.quantize_mx(out=h_w[:, cols].bitcast(FP8X4), scales=h_s[:, cols], in_=hb[q, lo][:])
+        def quantize_h(k):
+            lo, hi = PIECES[k]
+            nc.vector.quantize_mx(out=h_w[:, lo:hi].bitcast(FP8X4), scales=h_s[:, lo:hi], in_=hb[k][:])
 
         def logits(res, u0, j0, engine, bank_no):
             count, n = res.shape[1], res.shape[2]
@@ -223,47 +231,55 @@ def tile_list_transducer_joint_logits_kernel(
             rows = slice(u0 * P, (u0 + count) * P)
             nc.sync.dma_start(out=out[rows, j0 : j0 + n].rearrange("(e p) j -> p e j", p=P), in_=res[:])
 
-        def store(u0, j0, n, plan):
+        def store(u0, j0, n, plan, res=None):
             per_bank = HALF // n
-            res = held.tile([P, per_bank * len(plan), n], F32, name="res%d_%d" % (u0, j0))
+            if res is None:
+                res = held.tile([P, per_bank * len(plan), n], F32, name="res%d_%d" % (u0, j0))
             for b, (engine, bank_no) in enumerate(plan):
                 logits(res[:, per_bank * b : per_bank * (b + 1), :], u0 + per_bank * b, j0, engine, bank_no)
             write_out(res, u0, j0)
+            return res
 
-        whole = [(0, QUARTER)]
-        halves = [(0, P), (P, QUARTER)]
-        finish_sums(0)
-        join_tanh(0)
-        finish_sums(1)
-        join_gain(0, halves)
-        quantize_h(0, halves)
-        last_scales = shared.tile([P, QUARTER // 4], I32, name="last_scales", align_bytes=64, offset=HB_AT[0] + 8 * P - QUARTER)
-        nc.vector.tensor_copy(last_scales[:], v_s[1, 3].bitcast(I32))
-        v_s[1, 3] = last_scales[:].bitcast(U8)
-        join_tanh(1)
-        join_gain(1, whole)
-        store(6, 0, QUARTER, [("S", 0), ("V", 1)])
-        quantize_h(1, whole)
-        finish_sums(2)
-        join_tanh(2)
+        for k in (0, 1):
+            finish_sums(k)
+            join_tanh(k)
+        join_gain(0)
+        join_gain(1)
+        quantize_h(0)
+        quantize_h(1)
+        for k in (2, 3):
+            finish_sums(k)
+            join_tanh(k)
+        store(6, 0, QUARTER, [("S", 0)])
+        join_gain(2)
+        join_gain(3)
+        quantize_h(2)
+        quantize_h(3)
+        res_y = shared.tile([P, 2, QUARTER], F32, name="res_y", align_bytes=64, offset=RES_Y_AT)
+        store(8, 0, QUARTER, [("V", 1)], res_y)
+        finish_sums(4)
+        join_tanh(4)
         store(0, 0, HALF, [("S", 2)])
-        third = held.tile([P, 2, HALF], F32, name="third")
-        logits(third[:, 0:1, :], 1, 0, "V", 3)
-        finish_sums(3)
-        join_tanh(3)
-        join_gain(2, whole)
-        join_gain(3, whole)
-        quantize_h(2, whole)
-        quantize_h(3, whole)
-        logits(third[:, 1:2, :], 2, 0, "S", 0)
-        write_out(third, 1, 0)
-        store(3, 0, HALF, [("S", 1), ("S", 4)])
-        store(5, 0, HALF, [("S", 5)])
-        store(0, HALF, HALF, [("V", 6), ("S", 7)])
-        store(2, HALF, HALF, [("V", 0), ("S", 1), ("V", 4), ("S", 5)])
+        join_gain(4)
+        store(1, 0, HALF, [("V", 3)])
+        finish_sums(5)
+        join_tanh(5)
+        quantize_h(4)
+        join_gain(5)
+        quantize_h(5)
+        store(2, 0, HALF, [("S", 0)])
+        store(3, 0, HALF, [("S", 4)])
+        for u, wide, narrow in ((4, 5, 1), (5, 2, 3)):
+            long_res = held.tile([P, 1, HALF + QUARTER], F32, name="long_res%d" % u)
+            logits(long_res[:, :, 0:HALF], u, 0, "S", wide)
+            logits(long_res[:, :, HALF:], u, HALF, "V", narrow)
+            write_out(long_res, u, 0)
         rest = held.tile([P, 4, S - QUARTER], F32, name="rest")
-        logits(rest[:, 0:2, 0:QUARTER], 6, QUARTER, "V", 2)
+        store(4, HALF + QUARTER, QUARTER, [("V", 6)])
+        store(0, HALF, HALF, [("S", 7), ("V", 0)])
+        logits(rest[:, 0:2, 0:QUARTER], 6, QUARTER, "S", 5)
+        store(2, HALF, HALF, [("S", 4), ("V", 1)])
         for e in range(4):
-            logits(rest[:, e : e + 1, QUARTER:], 6 + e, HALF, "VS"[e % 2], (6, 7, 0, 1)[e])
-        logits(rest[:, 2:4, 0:QUARTER], 8, QUARTER, "V", 4)
+            logits(rest[:, e : e + 1, QUARTER:], 6 + e, HALF, "SVSV"[e], (2, 3, 6, 7)[e])
+        logits(rest[:, 2:4, 0:QUARTER], 8, QUARTER, "S", 5)
         write_out(rest, 6, QUARTER)

@@ -25,6 +25,7 @@ CAST_SPLIT = (44, 64)
 WF_AT = (10240, 18432)
 PIECES = ((0, 128), (128, 256), (256, 384), (384, 512), (512, 768), (768, 1024))
 FIRST_BANK = (0, 1, 2, 3, 4, 6)
+WARM_PASSES = 4
 HB_AT = (2048, 3072, 2048, 4096, 5120, 7168)
 RES_Y_AT = 2048 - 1024
 
@@ -147,16 +148,28 @@ def tile_list_transducer_joint_logits_kernel(
                     stop=stop and (t, c) == steps[-1],
                 )
 
+        warm_bank = psum.tile([P, HALF], F32, name="warm_bank", tag="bank7")
+        for w in range(WARM_PASSES):
+            nc.tensor.matmul_mx(
+                out=warm_bank[:],
+                lhsT=tab_w[0][:, 0:P].bitcast(FP8X4),
+                lhsT_scale=tab_s[:].bitcast(U8)[:, 0:P],
+                rhs=tab_w[0][:, 0:HALF].bitcast(FP8X4),
+                rhs_scale=tab_s[:].bitcast(U8)[:, 0:HALF],
+                start=True,
+                stop=True,
+            )
         gather_words(0, held.tile([P, HALF], U32, name="v_w00", align_bytes=64), 0, HALF)
-        nc.vector.tensor_copy(
-            out=wc_w[:].bitcast(U16),
-            in_=wc_raw[:].bitcast(U16).rearrange("p a (m t) -> p a t m", t=4),
-        )
         wc_s = held.tile([P, PASSES, 4, P], U8, name="wc_s", align_bytes=64)
-        nc.vector.tensor_copy(
-            out=wc_s[:],
-            in_=wc_s_raw[:].bitcast(U8).rearrange("p (a m t) -> p a t m", a=PASSES, t=4),
-        )
+        for a in range(PASSES):
+            nc.vector.tensor_copy(
+                out=wc_w[:, a, :, :].bitcast(U16),
+                in_=wc_raw[:, a, :].bitcast(U16).rearrange("p (m t) -> p t m", t=4),
+            )
+            nc.vector.tensor_copy(
+                out=wc_s[:, a, :, :],
+                in_=wc_s_raw[:].bitcast(U8)[:, a * H : (a + 1) * H].rearrange("p (m t) -> p t m", t=4),
+            )
         gather_words(0, shared.tile([P, HALF], U32, name="v_w01", align_bytes=64, offset=0), HALF, HALF)
         banks = [(k, b) for k in range(len(PIECES)) for b in range(len(bank_tiles(k)))]
         for k, b in banks:

@@ -21,11 +21,12 @@ PASSES = 2
 HALF = 512
 QUARTER = 256
 N_TILES = N // P
-CAST_SPLIT = (44, 64)
+CAST_SPLIT = (32, 76)
 WF_AT = (10240, 18432)
 PIECES = ((0, 128), (128, 256), (256, 384), (384, 512), (512, 768), (768, 1024))
 FIRST_BANK = (0, 1, 2, 3, 4, 6)
 WARM_PASSES = 4
+NARROW_FROM = 6
 HB_AT = (2048, 3072, 2048, 4096, 5120, 7168)
 RES_Y_AT = 2048 - 1024
 
@@ -86,11 +87,19 @@ def tile_list_transducer_joint_logits_kernel(
         v_s = [v_s0[:], v_s1[:].bitcast(U8)]
         gain_sb = held.tile([P, 4], F32, name="gain_sb")
         nc.sync.dma_start(out=gain_sb[:], in_=gain.rearrange("(p t) -> p t", t=4))
+        bias_sb = {}
+
+        def load_bias(u0, u1):
+            part = held.tile([P, u1 - u0], F32, name="bias%d" % u0)
+            with nc.allow_non_contiguous_dma(reason="one bias value for each partition and output tile"):
+                nc.sync.dma_start(out=part[:], in_=bias[u0 * P : u1 * P].rearrange("(u p) -> p u", p=P))
+            for u in range(u0, u1):
+                bias_sb[u] = part[:, u - u0 :]
+
+        load_bias(NARROW_FROM, N_TILES)
         wj_w = held.tile([P, N], I32, name="wj_w", align_bytes=64)
         nc.sync.dma_start(out=wj_w[:], in_=wj_words[0].rearrange("p c i -> p (c i)").bitcast(I32))
-        bias_sb = held.tile([P, N_TILES], F32, name="bias_sb")
-        with nc.allow_non_contiguous_dma(reason="one bias value for each partition and output tile"):
-            nc.sync.dma_start(out=bias_sb[:], in_=bias.rearrange("(u p) -> p u", p=P))
+        load_bias(0, NARROW_FROM)
 
         v_w = {}
 
@@ -204,9 +213,9 @@ def tile_list_transducer_joint_logits_kernel(
             lo, hi = PIECES[k]
             hb[k] = shared.tile([P, 4 * (hi - lo)], BF16, name="hb%d" % k, align_bytes=64, offset=HB_AT[k])
             nc.vector.tensor_tensor(
-                out=hb[k][:].rearrange("p (c i t) -> p c t i", i=4, t=4),
-                in0=th[k][:].rearrange("p t (c i) -> p c t i", i=4),
-                in1=gain_sb[:].unsqueeze(1).unsqueeze(3).to_broadcast([P, (hi - lo) // 4, 4, 4]),
+                out=hb[k][:].rearrange("p (c i t) -> p c t i", i=2, t=4),
+                in0=th[k][:].rearrange("p t (c i) -> p c t i", i=2),
+                in1=gain_sb[:].unsqueeze(1).unsqueeze(3).to_broadcast([P, (hi - lo) // 2, 4, 2]),
                 op=ALU.mult,
             )
 
@@ -232,25 +241,25 @@ def tile_list_transducer_joint_logits_kernel(
                 nc.vector.tensor_tensor(
                     out=res,
                     in0=bank[:],
-                    in1=bias_sb[:, u0 : u0 + count].unsqueeze(2).to_broadcast([P, count, n]),
+                    in1=bias_sb[u0][:, 0:count].unsqueeze(2).to_broadcast([P, count, n]),
                     op=ALU.add,
                 )
             else:
                 for e in range(count):
-                    nc.scalar.activation(res[:, e, :], bank[:, e, :], ACT.Identity, bias=bias_sb[:, u0 + e : u0 + e + 1])
+                    nc.scalar.activation(res[:, e, :], bank[:, e, :], ACT.Identity, bias=bias_sb[u0 + e][:, 0:1])
 
-        def write_out(res, u0, j0):
+        def write_out(res, u0, j0, queue=nc.sync):
             count, n = res.shape[1], res.shape[2]
             rows = slice(u0 * P, (u0 + count) * P)
-            nc.sync.dma_start(out=out[rows, j0 : j0 + n].rearrange("(e p) j -> p e j", p=P), in_=res[:])
+            queue.dma_start(out=out[rows, j0 : j0 + n].rearrange("(e p) j -> p e j", p=P), in_=res[:])
 
-        def store(u0, j0, n, plan, res=None):
+        def store(u0, j0, n, plan, res=None, queue=nc.sync):
             per_bank = HALF // n
             if res is None:
                 res = held.tile([P, per_bank * len(plan), n], F32, name="res%d_%d" % (u0, j0))
             for b, (engine, bank_no) in enumerate(plan):
                 logits(res[:, per_bank * b : per_bank * (b + 1), :], u0 + per_bank * b, j0, engine, bank_no)
-            write_out(res, u0, j0)
+            write_out(res, u0, j0, queue)
             return res
 
         for k in (0, 1):
@@ -287,12 +296,13 @@ def tile_list_transducer_joint_logits_kernel(
             logits(long_res[:, :, 0:HALF], u, 0, "S", wide)
             logits(long_res[:, :, HALF:], u, HALF, "V", narrow)
             write_out(long_res, u, 0)
-        rest = held.tile([P, 4, S - QUARTER], F32, name="rest")
+        rest = [held.tile([P, 2, S - QUARTER], F32, name="rest%d" % i) for i in range(2)]
         store(4, HALF + QUARTER, QUARTER, [("V", 6)])
         store(0, HALF, HALF, [("S", 7), ("V", 0)])
-        logits(rest[:, 0:2, 0:QUARTER], 6, QUARTER, "S", 5)
-        store(2, HALF, HALF, [("S", 4), ("V", 1)])
+        logits(rest[0][:, :, 0:QUARTER], 6, QUARTER, "S", 5)
+        store(2, HALF, HALF, [("S", 4), ("V", 1)], queue=nc.scalar)
         for e in range(4):
-            logits(rest[:, e : e + 1, QUARTER:], 6 + e, HALF, "SVSV"[e], (2, 3, 6, 7)[e])
-        logits(rest[:, 2:4, 0:QUARTER], 8, QUARTER, "S", 5)
-        write_out(rest, 6, QUARTER)
+            logits(rest[e // 2][:, e % 2 : e % 2 + 1, QUARTER:], 6 + e, HALF, "SVSV"[e], (2, 3, 6, 7)[e])
+        write_out(rest[0], 6, QUARTER)
+        logits(rest[1][:, :, 0:QUARTER], 8, QUARTER, "S", 5)
+        write_out(rest[1], 8, QUARTER, nc.scalar)

@@ -21,7 +21,7 @@ PASSES = 2
 HALF = 512
 QUARTER = 256
 N_TILES = N // P
-CAST_SPLIT = (32, 76)
+CAST_SPLIT = (30, 74)
 WF_AT = (10240, 18432)
 PIECES = ((0, 128), (128, 256), (256, 384), (384, 512), (512, 768), (768, 1024))
 FIRST_BANK = (0, 1, 2, 3, 4, 6)
@@ -67,15 +67,15 @@ def tile_list_transducer_joint_logits_kernel(
             return w
 
         nc.sync.dma_start(offsets[:], offs)
-        enc_sb = held.tile([P, 4], F32, name="enc_sb")
-        nc.sync.dma_start(out=enc_sb[:], in_=enc.rearrange("(p t) -> p t", t=4))
+        wc_raw = held.tile([P, PASSES, H // 2], I32, name="wc_raw", align_bytes=64)
+        nc.sync.dma_start(out=wc_raw[:], in_=wc_words.bitcast(I32).rearrange("a p c -> p a c"))
         tab_rows = tab_scales.bitcast(I32).rearrange("a (q r) c -> r q a c", r=4)
         for r in range(4):
             nc.sync.dma_start(out=tab_s[r:P:16, :], in_=tab_rows[r])
         tab_w = [load_table_words(0)]
-        wc_raw = held.tile([P, PASSES, H // 2], I32, name="wc_raw", align_bytes=64)
-        nc.sync.dma_start(out=wc_raw[:], in_=wc_words.bitcast(I32).rearrange("a p c -> p a c"))
         load_scale_rows(nc.sync, wc_s_raw, wc_scales)
+        enc_sb = held.tile([P, 4], F32, name="enc_sb")
+        nc.sync.dma_start(out=enc_sb[:], in_=enc.rearrange("(p t) -> p t", t=4))
         wf_raw = [load_wf(0), load_wf(1)]
         tab_w.append(load_table_words(1))
 

@@ -21,13 +21,14 @@ PASSES = 2
 HALF = 512
 QUARTER = 256
 N_TILES = N // P
-CAST_SPLIT = (30, 74)
+CAST_SPLIT = 46
 WF_AT = (10240, 18432)
 PIECES = ((0, 128), (128, 256), (256, 384), (384, 512), (512, 768), (768, 1024))
 FIRST_BANK = (0, 1, 2, 3, 4, 6)
 WARM_PASSES = 4
 NARROW_FROM = 6
 HB_AT = (2048, 3072, 2048, 4096, 5120, 7168)
+ROUNDED_AT = (26624, 30720)
 RES_Y_AT = 2048 - 1024
 
 
@@ -74,8 +75,6 @@ def tile_list_transducer_joint_logits_kernel(
             nc.sync.dma_start(out=tab_s[r:P:16, :], in_=tab_rows[r])
         tab_w = [load_table_words(0)]
         load_scale_rows(nc.sync, wc_s_raw, wc_scales)
-        enc_sb = held.tile([P, 4], F32, name="enc_sb")
-        nc.sync.dma_start(out=enc_sb[:], in_=enc.rearrange("(p t) -> p t", t=4))
         wf_raw = [load_wf(0), load_wf(1)]
         tab_w.append(load_table_words(1))
 
@@ -85,6 +84,8 @@ def tile_list_transducer_joint_logits_kernel(
         for r in range(4):
             nc.sync.dma_start(out=v_s1[r:P:32, :], in_=v_s0[:].bitcast(I32)[16 + r : P : 32, :])
         v_s = [v_s0[:], v_s1[:].bitcast(U8)]
+        enc_sb = held.tile([P, 4], F32, name="enc_sb")
+        nc.sync.dma_start(out=enc_sb[:], in_=enc.rearrange("(p t) -> p t", t=4))
         gain_sb = held.tile([P, 4], F32, name="gain_sb")
         nc.sync.dma_start(out=gain_sb[:], in_=gain.rearrange("(p t) -> p t", t=4))
         bias_sb = {}
@@ -113,11 +114,15 @@ def tile_list_transducer_joint_logits_kernel(
         wf_s = [held.tile([P, 4, P], U8, name="wf_s%d" % a, align_bytes=64) for a in range(PASSES)]
 
         def quantize_wf(a):
-            rounded = held.tile([P, 4, P, 4], BF16, name="wf_bf%d" % a, align_bytes=64)
-            for copy, m0, m1 in ((nc.vector.tensor_copy, 0, CAST_SPLIT[a]), (nc.scalar.copy, CAST_SPLIT[a], P)):
+            rounded = shared.tile([P, 4, P, 4], BF16, name="wf_bf%d" % a, align_bytes=64, offset=ROUNDED_AT[a])
+            if a == 0:
+                shares = ((0, CAST_SPLIT, 0, 4), (CAST_SPLIT, P, 0, 4))
+            else:
+                shares = ((0, P, 0, 2), (0, P, 2, 4))
+            for copy, (m0, m1, t0, t1) in zip((nc.vector.tensor_copy, nc.scalar.copy), shares):
                 copy(
-                    out=rounded[:, :, m0:m1, :].rearrange("p t m j -> p m j t"),
-                    in_=wf_raw[a][:].rearrange("p j (m t) -> p m j t", t=4)[:, m0:m1, :, :],
+                    out=rounded[:, t0:t1, m0:m1, :].rearrange("p t m j -> p m j t"),
+                    in_=wf_raw[a][:].rearrange("p j (m t) -> p m j t", t=4)[:, m0:m1, :, t0:t1],
                 )
             for t0 in (0, 2):
                 nc.vector.quantize_mx(
@@ -187,7 +192,7 @@ def tile_list_transducer_joint_logits_kernel(
         for k, b in banks:
             project("fine", 0, k, b)
         quantize_wf(1)
-        wj_s = shared.tile([P, N // 4], I32, name="wj_s", align_bytes=64, offset=WF_AT[1])
+        wj_s = shared.tile([P, N // 4], I32, name="wj_s", align_bytes=64, offset=ROUNDED_AT[1] + 2048)
         nc.vector.memset(wj_s[:], 0)
         load_scale_rows(nc.scalar, wj_s, wj_scales)
         for q in range(4):

from contextlib import ExitStack

import concourse.mybir as mybir

K, H, N, T, S = 1024, 512, 1280, 2048, 1024
FLOPS = 2 * S * (2 * K * H + H * N)

F32 = mybir.dt.float32
BF16 = mybir.dt.bfloat16
I32 = mybir.dt.int32
U32 = mybir.dt.uint32
U16 = mybir.dt.uint16
U8 = mybir.dt.uint8
FP8X4 = mybir.dt.float8_e4m3fn_x4
FP4X4 = mybir.dt.float4_e2m1fn_x4
ACT = mybir.ActivationFunctionType
ALU = mybir.AluOpType

P = 128
PASSES = 2
HALF = 512
QUARTER = 256
N_TILES = N // P
CAST_SPLIT = 46
WF_AT = (10240, 18432)
PIECES = ((0, 128), (128, 256), (256, 384), (384, 512), (512, 768), (768, 1024))
FIRST_BANK = (0, 1, 2, 3, 4, 6)
WARM_PASSES = 4
NARROW_FROM = 6
HB_AT = (2048, 3072, 2048, 4096, 5120, 7168)
ROUNDED_AT = (26624, 30720)
RES_Y_AT = 2048 - 1024


def tile_list_transducer_joint_logits_kernel(
    tc, tab_words, tab_scales, offs, wc_words, wc_scales, wf, enc, gain, wj_words, wj_scales, bias, out
):
    nc = tc.nc
    with ExitStack() as ctx:
        held = ctx.enter_context(tc.tile_pool(name="held", bufs=1))
        psum = ctx.enter_context(tc.psum_pool(name="psum", bufs=1))
        shared = ctx.enter_context(tc.tile_pool(name="shared", bufs=1))

        offsets = held.tile([P, S // 16], U16, name="offsets")
        tab_s = held.tile([P, T // 4], I32, name="tab_s", align_bytes=64)
        wc_s_raw = shared.tile([P, PASSES * H // 4], I32, name="wc_s_raw", align_bytes=64, offset=0)
        v_s1 = held.tile([P, S // 4], I32, name="v_s1", align_bytes=64)
        warm = held.tile([P, 2], F32, name="warm")
        nc.gpsimd.memset(tab_s[:], 0)
        nc.vector.memset(warm[:, 0:1], 0.0)
        nc.vector.memset(wc_s_raw[:], 0)
        nc.vector.memset(v_s1[:], 0)
        nc.scalar.activation(warm[:, 1:2], warm[:, 0:1], ACT.Tanh)

        def load_scale_rows(queue, dst, src):
            rows = src.bitcast(I32).rearrange("a (q r) c -> r q a c", r=4)
            for r in range(4):
                queue.dma_start(out=dst[r:P:32, :].rearrange("q (a c) -> q a c", a=src.shape[0]), in_=rows[r])

        def load_table_words(a):
            words = held.tile([P, T], I32, name="tab_w%d" % a, align_bytes=64)
            nc.sync.dma_start(out=words[:], in_=tab_words[a].rearrange("p t i -> p (t i)").bitcast(I32))
            return words

        def load_wf(a):
            w = shared.tile([P, 4, H], F32, name="wf_raw%d" % a, align_bytes=64, offset=WF_AT[a])
            nc.sync.dma_start(out=w[:], in_=wf[512 * a : 512 * (a + 1), :].rearrange("(p j) c -> p j c", j=4))
            return w

        nc.sync.dma_start(offsets[:], offs)
        wc_raw = held.tile([P, PASSES, H // 2], I32, name="wc_raw", align_bytes=64)
        nc.sync.dma_start(out=wc_raw[:], in_=wc_words.bitcast(I32).rearrange("a p c -> p a c"))
        tab_rows = tab_scales.bitcast(I32).rearrange("a (q r) c -> r q a c", r=4)
        for r in range(4):
            nc.sync.dma_start(out=tab_s[r:P:16, :], in_=tab_rows[r])
        tab_w = [load_table_words(0)]
        load_scale_rows(nc.sync, wc_s_raw, wc_scales)
        wf_raw = [load_wf(0), load_wf(1)]
        tab_w.append(load_table_words(1))

        wc_w = held.tile([P, PASSES, 4, 2 * P], U8, name="wc_w", align_bytes=64)
        v_s0 = held.tile([P, S], U8, name="v_s0", align_bytes=64)
        nc.vector.tensor_copy(v_s0[:], tab_s[:].bitcast(U8).indirect(offsets[:]))
        for r in range(4):
            nc.sync.dma_start(out=v_s1[r:P:32, :], in_=v_s0[:].bitcast(I32)[16 + r : P : 32, :])
        v_s = [v_s0[:], v_s1[:].bitcast(U8)]
        enc_sb = held.tile([P, 4], F32, name="enc_sb")
        nc.sync.dma_start(out=enc_sb[:], in_=enc.rearrange("(p t) -> p t", t=4))
        gain_sb = held.tile([P, 4], F32, name="gain_sb")
        nc.sync.dma_start(out=gain_sb[:], in_=gain.rearrange("(p t) -> p t", t=4))
        bias_sb = {}

        def load_bias(u0, u1):
            part = held.tile([P, u1 - u0], F32, name="bias%d" % u0)
            with nc.allow_non_contiguous_dma(reason="one bias value for each partition and output tile"):
                nc.sync.dma_start(out=part[:], in_=bias[u0 * P : u1 * P].rearrange("(u p) -> p u", p=P))
            for u in range(u0, u1):
                bias_sb[u] = part[:, u - u0 :]

        load_bias(NARROW_FROM, N_TILES)
        wj_w = held.tile([P, N], I32, name="wj_w", align_bytes=64)
        nc.sync.dma_start(out=wj_w[:], in_=wj_words[0].rearrange("p c i -> p (c i)").bitcast(I32))
        load_bias(0, NARROW_FROM)

        v_w = {}

        def gather_words(a, dst, j0, n):
            nc.vector.tensor_copy(dst[:], tab_w[a][:].bitcast(U32).indirect(offsets[:, j0 // 16 : (j0 + n) // 16]))
            for k, (lo, hi) in enumerate(PIECES):
                if j0 <= lo and hi <= j0 + n:
                    v_w[a, k] = dst[:, lo - j0 : hi - j0]

        wf_w = [held.tile([P, 4, P], U32, name="wf_w%d" % a, align_bytes=64) for a in range(PASSES)]
        wf_s = [held.tile([P, 4, P], U8, name="wf_s%d" % a, align_bytes=64) for a in range(PASSES)]

        def quantize_wf(a):
            rounded = shared.tile([P, 4, P, 4], BF16, name="wf_bf%d" % a, align_bytes=64, offset=ROUNDED_AT[a])
            if a == 0:
                shares = ((0, CAST_SPLIT, 0, 4), (CAST_SPLIT, P, 0, 4))
            else:
                shares = ((0, P, 0, 2), (0, P, 2, 4))
            for copy, (m0, m1, t0, t1) in zip((nc.vector.tensor_copy, nc.scalar.copy), shares):
                copy(
                    out=rounded[:, t0:t1, m0:m1, :].rearrange("p t m j -> p m j t"),
                    in_=wf_raw[a][:].rearrange("p j (m t) -> p m j t", t=4)[:, m0:m1, :, t0:t1],
                )
            for t0 in (0, 2):
                nc.vector.quantize_mx(
                    out=wf_w[a][:, t0 : t0 + 2, :].rearrange("p t m -> p (t m)").bitcast(FP8X4),
                    scales=wf_s[a][:, t0 : t0 + 2, :].rearrange("p t m -> p (t m)"),
                    in_=rounded[:, t0 : t0 + 2, :, :].rearrange("p t m j -> p (t m j)"),
                )

        sums = {}

        def bank_tiles(k):
            lo, hi = PIECES[k]
            per_bank = HALF // (hi - lo)
            return [range(t0, t0 + per_bank) for t0 in range(0, 4, per_bank)]

        def project(kind, a, k, b, start=False, stop=False):
            lo, hi = PIECES[k]
            tiles = bank_tiles(k)[b]
            if start:
                bank = psum.tile([P, len(tiles), hi - lo], F32, name="sums", tag="bank%d" % (FIRST_BANK[k] + b))
                for e, t in enumerate(tiles):
                    sums[k, t] = bank[:, e, :]
            n = P if kind == "coarse" else hi - lo
            steps = [(t, c) for t in tiles for c in range(0, hi - lo, n)]
            for t, c in steps:
                if kind == "coarse":
                    lhsT, lhsT_scale = wc_w[:, a, t, :].bitcast(FP4X4), wc_s[:, a, t, :]
                else:
                    lhsT, lhsT_scale = wf_w[a][:, t, :].bitcast(FP8X4), wf_s[a][:, t, :]
                nc.tensor.matmul_mx(
                    out=sums[k, t][:, c : c + n],
                    lhsT=lhsT,
                    lhsT_scale=lhsT_scale,
                    rhs=v_w[a, k][:, c : c + n].bitcast(FP8X4),
                    rhs_scale=v_s[a][:, lo + c : lo + c + n],
                    start=start and (t, c) == steps[0],
                    stop=stop and (t, c) == steps[-1],
                )

        warm_bank = psum.tile([P, HALF], F32, name="warm_bank", tag="bank7")
        for w in range(WARM_PASSES):
            nc.tensor.matmul_mx(
                out=warm_bank[:],
                lhsT=tab_w[0][:, 0:P].bitcast(FP8X4),
                lhsT_scale=tab_s[:].bitcast(U8)[:, 0:P],
                rhs=tab_w[0][:, 0:HALF].bitcast(FP8X4),
                rhs_scale=tab_s[:].bitcast(U8)[:, 0:HALF],
                start=True,
                stop=True,
            )
        gather_words(0, held.tile([P, HALF], U32, name="v_w00", align_bytes=64), 0, HALF)
        wc_s = held.tile([P, PASSES, 4, P], U8, name="wc_s", align_bytes=64)
        for a in range(PASSES):
            nc.vector.tensor_copy(
                out=wc_w[:, a, :, :].bitcast(U16),
                in_=wc_raw[:, a, :].bitcast(U16).rearrange("p (m t) -> p t m", t=4),
            )
            nc.vector.tensor_copy(
                out=wc_s[:, a, :, :],
                in_=wc_s_raw[:].bitcast(U8)[:, a * H : (a + 1) * H].rearrange("p (m t) -> p t m", t=4),
            )
        gather_words(0, shared.tile([P, HALF], U32, name="v_w01", align_bytes=64, offset=0), HALF, HALF)
        banks = [(k, b) for k in range(len(PIECES)) for b in range(len(bank_tiles(k)))]
        for k, b in banks:
            project("coarse", 0, k, b, start=True)
        quantize_wf(0)
        for k, b in banks:
            project("fine", 0, k, b)
        quantize_wf(1)
        wj_s = shared.tile([P, N // 4], I32, name="wj_s", align_bytes=64, offset=ROUNDED_AT[1] + 2048)
        nc.vector.memset(wj_s[:], 0)
        load_scale_rows(nc.scalar, wj_s, wj_scales)
        for q in range(4):
            gather_words(1, held.tile([P, QUARTER], U32, name="v_w1%d" % q, align_bytes=64), q * QUARTER, QUARTER)

        def finish_sums(k):
            for b in range(len(bank_tiles(k))):
                project("coarse", 1, k, b)
                project("fine", 1, k, b, stop=True)

        h_w = held.tile([P, S], U32, name="h_w", align_bytes=64)
        h_s = held.tile([P, S], U8, name="h_s", align_bytes=64)
        th = {}
        hb = {}

        def join_tanh(k):
            lo, hi = PIECES[k]
            th[k] = held.tile([P, 4, hi - lo], F32, name="th%d" % k, align_bytes=64)
            for t in range(4):
                nc.scalar.activation(th[k][:, t, :], sums[k, t], ACT.Tanh, bias=enc_sb[:, t : t + 1])

        def join_gain(k):
            lo, hi = PIECES[k]
            hb[k] = shared.tile([P, 4 * (hi - lo)], BF16, name="hb%d" % k, align_bytes=64, offset=HB_AT[k])
            nc.vector.tensor_tensor(
                out=hb[k][:].rearrange("p (c i t) -> p c t i", i=2, t=4),
                in0=th[k][:].rearrange("p t (c i) -> p c t i", i=2),
                in1=gain_sb[:].unsqueeze(1).unsqueeze(3).to_broadcast([P, (hi - lo) // 2, 4, 2]),
                op=ALU.mult,
            )

        def quantize_h(k):
            lo, hi = PIECES[k]
            nc.vector.quantize_mx(out=h_w[:, lo:hi].bitcast(FP8X4), scales=h_s[:, lo:hi], in_=hb[k][:])

        def logits(res, u0, j0, engine, bank_no):
            count, n = res.shape[1], res.shape[2]
            bank = psum.tile([P, count, n], F32, name="bank", tag="bank%d" % bank_no)
            for e in range(count):
                u = u0 + e
                nc.tensor.matmul_mx(
                    out=bank[:, e, :],
                    lhsT=wj_w[:, u * P : (u + 1) * P].bitcast(FP8X4),
                    lhsT_scale=wj_s[:].bitcast(U8)[:, u * P : (u + 1) * P],
                    rhs=h_w[:, j0 : j0 + n].bitcast(FP8X4),
                    rhs_scale=h_s[:, j0 : j0 + n],
                    start=True,
                    stop=True,
                )
            if engine == "V":
                nc.vector.tensor_tensor(
                    out=res,
                    in0=bank[:],
                    in1=bias_sb[u0][:, 0:count].unsqueeze(2).to_broadcast([P, count, n]),
                    op=ALU.add,
                )
            else:
                for e in range(count):
                    nc.scalar.activation(res[:, e, :], bank[:, e, :], ACT.Identity, bias=bias_sb[u0 + e][:, 0:1])

        def write_out(res, u0, j0, queue=nc.sync):
            count, n = res.shape[1], res.shape[2]
            rows = slice(u0 * P, (u0 + count) * P)
            queue.dma_start(out=out[rows, j0 : j0 + n].rearrange("(e p) j -> p e j", p=P), in_=res[:])

        def store(u0, j0, n, plan, res=None, queue=nc.sync):
            per_bank = HALF // n
            if res is None:
                res = held.tile([P, per_bank * len(plan), n], F32, name="res%d_%d" % (u0, j0))
            for b, (engine, bank_no) in enumerate(plan):
                logits(res[:, per_bank * b : per_bank * (b + 1), :], u0 + per_bank * b, j0, engine, bank_no)
            write_out(res, u0, j0, queue)
            return res

        for k in (0, 1):
            finish_sums(k)
            join_tanh(k)
        join_gain(0)
        join_gain(1)
        quantize_h(0)
        quantize_h(1)
        for k in (2, 3):
            finish_sums(k)
            join_tanh(k)
        store(6, 0, QUARTER, [("S", 0)])
        join_gain(2)
        join_gain(3)
        quantize_h(2)
        quantize_h(3)
        res_y = shared.tile([P, 2, QUARTER], F32, name="res_y", align_bytes=64, offset=RES_Y_AT)
        store(8, 0, QUARTER, [("V", 1)], res_y)
        finish_sums(4)
        join_tanh(4)
        store(0, 0, HALF, [("S", 2)])
        join_gain(4)
        store(1, 0, HALF, [("V", 3)])
        finish_sums(5)
        join_tanh(5)
        quantize_h(4)
        join_gain(5)
        quantize_h(5)
        store(2, 0, HALF, [("S", 0)])
        store(3, 0, HALF, [("S", 4)])
        for u, wide, narrow in ((4, 5, 1), (5, 2, 3)):
            long_res = held.tile([P, 1, HALF + QUARTER], F32, name="long_res%d" % u)
            logits(long_res[:, :, 0:HALF], u, 0, "S", wide)
            logits(long_res[:, :, HALF:], u, HALF, "V", narrow)
            write_out(long_res, u, 0)
        rest = [held.tile([P, 2, S - QUARTER], F32, name="rest%d" % i) for i in range(2)]
        store(4, HALF + QUARTER, QUARTER, [("V", 6)])
        store(0, HALF, HALF, [("S", 7), ("V", 0)])
        logits(rest[0][:, :, 0:QUARTER], 6, QUARTER, "S", 5)
        store(2, HALF, HALF, [("S", 4), ("V", 1)], queue=nc.scalar)
        for e in range(4):
            logits(rest[e // 2][:, e % 2 : e % 2 + 1, QUARTER:], 6 + e, HALF, "SVSV"[e], (2, 3, 6, 7)[e])
        write_out(rest[0], 6, QUARTER)
        logits(rest[1][:, :, 0:QUARTER], 8, QUARTER, "S", 5)
        write_out(rest[1], 8, QUARTER, nc.scalar)
